import numpy as np, ml_dtypes
CORES = [2,6,10,14,18,22,26,30]
N = 8
import mx_ref
BF = ml_dtypes.bfloat16
def gentries(a):
    return np.ascontiguousarray(a.reshape(8, 16, -1).transpose(0, 2, 1)).reshape(8, -1)
def gtable(e):
    e = np.asarray(e); return np.ascontiguousarray(e.reshape(8, -1, 16).transpose(0, 2, 1)).reshape(128, -1).astype(np.int32)
def gcols(t, e):
    v = np.concatenate([t.reshape(8, 16, -1, 4), np.zeros((8, 16, 1, 4), BF)], axis=2)
    return np.ascontiguousarray(np.stack([v[g][:, e[g]] for g in range(8)])).reshape(128, -1)
def tile(rs):
    return np.stack(rs, axis=2).reshape(128, -1).astype(BF)
def cut(t, i, w=512):
    return t[:, w * i:w * i + w]
def pick(q, e):
    c = np.concatenate([q[0].reshape(128, -1, 4), np.zeros((128, 1, 4), np.uint8)], axis=1); s = np.concatenate([q[1], np.ones((16, 1), np.uint8)], axis=1)
    return (np.ascontiguousarray(c[:, e].reshape(128, -1)), np.ascontiguousarray(s[:, e]))
def join(*qs):
    return (np.concatenate([q[0] for q in qs], axis=1), np.concatenate([q[1] for q in qs], axis=1))
def put(q, e, v):
    c, s = q[0].reshape(128, -1, 4).copy(), q[1].copy(); c[:, e] = v[0].reshape(128, -1, 4); s[:, e] = v[1]
    return (c.reshape(128, -1), s)
def pk(c, s):
    return (np.ascontiguousarray(c), mx_ref.live(s))
def emit(q):
    return q[0], q[1]
def packed(v, rng):
    q = [mx_ref.quantize(np.ascontiguousarray(v[r])) for r in range(N)]
    return np.stack([a for a, b in q]), np.stack([mx_ref.plane(b, rng) for a, b in q])
def values_of_codes():
    e, c = np.zeros((128, 128, 4), np.float32), np.zeros((128, 2, 4), np.uint8)
    e[np.arange(128), np.arange(128), 0] = 1
    c[:127, :, 0] = np.arange(256).reshape(2, 128).T[:127]
    return mx_ref.matmul(mx_ref.quantize(e.reshape(128, 512).astype(BF)), (c.reshape(128, 8), np.full((16, 2), 127, np.uint8))).T.reshape(-1).astype(np.float64)
CODE_VALUE, SCALE_VALUE = values_of_codes(), 2.0 ** (np.arange(256) - 127.0)
def decode(q):
    return (CODE_VALUE[q[0]].reshape(16, 8, -1, 4) * SCALE_VALUE[q[1]][:, None, :, None] + 0.0).reshape(128, -1).astype(np.float32)
def f(rng, *shape):
    return mx_ref.flush((rng.standard_normal(shape, dtype=np.float32) * np.exp2(rng.integers(-2, 3, shape[:-1] + (1,)))).astype(BF))
def wide(rng, *shape, cols=0):
    v = rng.standard_normal(shape, dtype=np.float32) * np.exp2(rng.integers(-12, 13, shape)).astype(np.float32)
    if cols: v *= np.repeat(np.exp2(rng.integers(-cols, cols + 1, shape[:-2] + (1, shape[-1] // 4))) * (rng.random(shape[:-2] + (1, shape[-1] // 4)) > 0.0625), 4, axis=-1).astype(np.float32)
    return mx_ref.flush(v.astype(BF))
C, K, M, R, S = 384, 96, 3, 3, 4
def order(p):
    return np.argsort(-(p[::16] + np.float32(0.0)), axis=1, kind="stable")
def replies(o, m):
    place = np.argsort(o, axis=1)
    label = np.where(place >= C - K, 2, 0)
    when = np.zeros((8, C), int)
    for n in range(1, S + 1):
        to = np.take_along_axis(label, m, axis=1).reshape(8, M, C)
        won = (label == 0) & (to == 2).any(axis=1)
        lost = (label == 0) & (to == 1).all(axis=1)
        when[won | lost] = n
        label[won] = 1
        label[lost] = 2
    to = np.take_along_axis(label, m, axis=1).reshape(8, M, C)
    at = np.take_along_axis(when, m, axis=1).reshape(8, M, C)
    best = np.argmin(np.take_along_axis(place, m, axis=1).reshape(8, M, C), axis=1)
    k = np.where(label == 1, np.argmin(np.where(to == 2, at, S + 1), axis=1), np.where(label == 2, np.argmax(np.where(to == 1, at, -1), axis=1), best))
    t = np.take_along_axis(m.reshape(8, M, C), k[:, None], axis=1)[:, 0]
    return np.concatenate([np.where(place >= C - K, place + K, t), np.tile(C + np.arange(K), (8, 1))], axis=1)
def big(v):
    v = v.astype(np.float32)
    v[np.abs(v) < np.float32(2.0 ** -16)] = 0
    return v.astype(BF)
def numbers_of(rng):
    return {"x": big(f(rng, N, 128, 4 * C)), "u": np.array(f(rng, N, 128, 512)), "v": np.array(f(rng, N, 128, 512))}
def moves(rng):
    return np.stack([gtable(rng.integers(0, C, (8, M * C))) for r in range(N)])
def weights(rng, w):
    c, p = packed(w, rng)
    return {"wc": c, "ws": p}
def within(rng, a, b):
    w = np.array(f(rng, N, 128, 2048)).reshape(N, 8, 16, 4, 8, 16, 4)
    z = np.zeros_like(w)
    z[:, :, a:b, :, :, a:b] = w[:, :, a:b, :, :, a:b]
    return weights(rng, z.reshape(N, 128, 2048))
def signs(rng):
    return np.stack([rng.permutation(8) % 2 * 2.0 - 1.0 for r in range(N)])
def lead(rng, m, i, one, others):
    m[:, i] = rng.choice(others, (M, len(i)))
    m[rng.integers(0, M, len(i)), i] = rng.choice(one, len(i))
def game(rng, dead, rest, kind, g):
    m = rng.integers(0, C, (M, C))
    a, b, c, d, e, h = np.array_split(rng.permutation(rest), 6)
    if kind == 0:
        lead(rng, m, a, dead, np.arange(C))
        lead(rng, m, b, a, a)
        lead(rng, m, c, b, rest)
        lead(rng, m, d, c, np.concatenate([a, c]))
        lead(rng, m, e, d, np.concatenate([a, c, d, e]))
        lead(rng, m, h, h, np.concatenate([a, c, h]))
    elif kind == 1:
        lead(rng, m, rest, rest, rest)
        z = np.sort(rest[:C - 2 * K])[-2:]
        i = rng.choice(rest, 8)
        m[0, i] = z[1]
        m[1:, i] = z[0]
    elif kind == 2 and g % 2: lead(rng, m, rest, dead, np.arange(C))
    elif kind == 2: m[:] = dead[0]
    else:
        lead(rng, m, a, dead, np.arange(C))
        lead(rng, m, np.concatenate([b, c, d, e, h]), a, a)
    return m
def setup_inputs(rng):
    return {**numbers_of(rng), "mv": moves(rng), **weights(rng, f(rng, N, 128, 2048))}
def setup_inputs_ties(rng):
    d = numbers_of(rng)
    e = rng.permutation(N)
    x = d["x"].reshape(N, 8, 16, C, 4)
    for r in range(N):
        k = np.zeros(C, int) if r == e[0] else rng.permutation(C) % 3
        a = x[r][:, :8, :3].copy()
        a[:, :, 2] = 0
        x[r][:, :8] = a[:, :, k]
    x[e[1]] = 0
    u = d["u"].reshape(N, 8, 16, 128, 4)
    u[:, :, 8:, ::16] = 0
    w = np.array(f(rng, N, 128, 2048)).reshape(N, 8, 16, 4, 8, 16, 4)
    w[:, :, 8:, :, :, :8] = 0
    return {"x": x.reshape(N, 128, 4 * C), "u": u.reshape(N, 128, 512), "v": d["v"], "mv": moves(rng), **weights(rng, w.reshape(N, 128, 2048))}
def setup_inputs_near(rng):
    d = numbers_of(rng)
    x = d["x"].astype(np.float32).reshape(N, 8, 16, C, 4)
    s = np.arange(C) // 2
    g = ((s[:, None] >> np.arange(8)) & 1) * np.exp2(np.arange(8) - 23.0)
    c = np.stack([rng.permutation(8) for r in range(N)])
    z = c % 2 * 2.0 - 1.0
    x[:, :, 0] = 0
    x[:, :, 0, :, 0] = z[:, :, None]
    j = rng.integers(0, C, N)
    x[np.arange(N)[:, None], np.arange(8), 0, j[:, None], 0] = np.where(z > 0, 2.0 ** 30, np.where(c % 4 == 0, -2.0 ** 30, -1.0))
    x[:, :, 8] = g[:, :4]
    x[:, :, 9] = g[:, 4:]
    x[:, :, 10:] = rng.integers(4, 8, (N, 8, 6, C, 4)) * rng.choice([-1.0, 1.0], (N, 8, 6, C, 4)) * 2.0 ** -20
    u = d["u"].reshape(N, 128, 128, 4)
    k = np.where(rng.permutation(N) < N // 2, 2.0 ** -30, 1.0).astype(np.float32).astype(BF)
    u[:, :, ::16] = 0
    for h in range(0, 128, 16):
        u[:, h, h, 0] = k
        u[:, h + 8:h + 10, h] = k[:, None, None]
    return {"x": x.reshape(N, 128, 4 * C).astype(BF), "u": u.reshape(N, 128, 512), "v": d["v"], "mv": moves(rng), **within(rng, 1, 8)}
def setup_inputs_waves(rng):
    d = numbers_of(rng)
    o = rng.permutation(N)
    small = rng.permutation(N) < N // 2
    c = np.zeros((N, 8, C))
    m = []
    for r in range(N):
        own = []
        for g in range(8):
            e = rng.permutation(C)
            c[r, g, e[:K]] = -1
            c[r, g, e[C - K:]] = 1
            own.append(game(rng, e[:K], e[K:], o[r] % 4, g).reshape(-1))
        m.append(gtable(np.stack(own)))
    k = np.where(small, 2.0 ** -30, 1.0).astype(np.float32)
    x = d["x"].reshape(N, 8, 16, C, 4)
    x[:, :, :8] = 0
    x[:, :, 0, :, 0] = ((2.5 * np.abs(c) + 0.5 * c) * k[:, None, None]).astype(np.float32).astype(BF)
    x[:, :, 1, :, 0] = ((2.5 * np.abs(c) - 0.5 * c) * k[:, None, None]).astype(np.float32).astype(BF)
    u = d["u"].reshape(N, 128, 128, 4)
    u[:, :, ::16] = 0
    for h in range(0, 128, 16):
        u[:, h, h, 0] = k.astype(BF)
        u[:, h + 1, h, 0] = (-k).astype(BF)
    return {"x": x.reshape(N, 128, 4 * C), "u": u.reshape(N, 128, 512), "v": d["v"], "mv": np.stack(m), **within(rng, 8, 16)}
def setup_inputs_huge(rng):
    d = numbers_of(rng)
    x = 2.0 ** 29 * (0.8 + 0.2 * rng.random((N, 128, C, 4)))
    c = np.stack([rng.permutation(C) % 2 * 2.0 - 1.0 for r in range(N)])
    c[rng.permutation(N) < N // 2] = 1
    x *= c[:, None, :, None]
    u = d["u"].reshape(N, 128, 128, 4)
    a = 2.0 ** 30 * (1 - 0.25 * rng.random((N, 128, 8, 4))) * signs(rng)[:, None, :, None]
    u[:, :, ::16] = a.astype(np.float32).astype(BF)
    w = np.zeros((N, 128, 4, 128, 4), np.float32)
    i = np.arange(128)
    for b in range(4): w[:, i, b, i, b] = 4
    return {"x": x.astype(np.float32).reshape(N, 128, 4 * C).astype(BF), "u": u.reshape(N, 128, 512), "v": d["v"], "mv": moves(rng), **weights(rng, w.reshape(N, 128, 2048).astype(BF))}
def setup_inputs_spread(rng):
    d = setup_inputs(rng)
    d["x"] = big(wide(rng, N, 128, 4 * C, cols=6))
    return d
def check_inputs(d):
    b = []
    for k in ("x", "u", "v"):
        a = np.abs(d[k].astype(np.float32))
        if not (np.isfinite(a).all() and ((a == 0) | (a >= 2.0 ** -30) & (a <= 2.0 ** 30)).all()): b.append("a value of " + k)
    if ((d["mv"] < 0) | (d["mv"] >= C)).any(): b.append("an entry of mv")
    if (d["wc"] % 128 == 127).any(): b.append("a code of wc")
    none, low, high = [np.max(s) for c, s in [mx_ref.quantize(np.full((128, 16), k).astype(BF)) for k in (0.0, 2.0 ** -30, 2.0 ** 30)]]
    live = np.stack([mx_ref.live(p) for p in d["ws"]])
    if ((live != none) & ((live < low) | (live > high))).any(): b.append("a scale of ws")
    return b
def reference(x, u, v, mv, wc, ws):
    qu = [mx_ref.quantize(u[r]) for r in range(N)]
    lay = [pk(wc[r], ws[r]) for r in range(N)]
    now = [x[r] for r in range(N)]
    to = [None] * N
    for n in range(R):
        border = []
        for r in range(N):
            o = order(mx_ref.matmul(qu[r], mx_ref.quantize(now[r])))
            border.append(mx_ref.quantize(gcols(now[r], o[:, :K])))
            to[r] = replies(o, gentries(mv[r]))
        came = decode(join(*border)).astype(BF)
        for r in range(N):
            both = np.concatenate([now[r], cut(came, (r + 1) % N, 4 * K)], axis=1)
            t = to[r][:, :C]
            one = gcols(both, t).astype(np.float32)
            two = gcols(both, np.take_along_axis(to[r], t, axis=1)).astype(np.float32)
            q = mx_ref.quantize(((one + two) * np.float32(0.5)).astype(BF))
            old = now[r].astype(np.float32)
            now[r] = tile([old[:, b::4] + mx_ref.matmul(pick(lay[r], np.arange(128 * b, 128 * b + 128)), q) * np.float32(0.03125) for b in range(4)])
    y, ot = np.zeros((N, 128, C), np.float32), np.zeros((N, 8, C), np.float32)
    oc, osc = np.zeros((N, 128, 4 * C), np.uint8), np.zeros((N, 16, C), np.uint8)
    for r in range(N):
        q = mx_ref.quantize(now[r])
        y[r] = mx_ref.matmul(mx_ref.quantize(v[r]), q)
        ot[r] = to[r][:, :C]
        oc[r], osc[r] = emit(q)
    return {"y": y, "ot": ot, "oc": oc, "osc": osc}

@@ -1,0 +1,510 @@
+import numpy as np
+from concourse.mybir import dt, AluOpType, ActivationFunctionType
+
+C, K, ROUNDS = 384, 96, 3
+FW = C + K
+H = 256
+STEP = 2.0 ** -10
+YB = 1.625
+CUT = YB + (C - K - 0.5) * STEP
+U = float(2 ** 21)
+PREF = 512.0
+BIG = float(2 ** 26)
+FILL = 15000000
+TINY = 2.0 ** -120
+X4, U8, BF, F32, I32, U16 = "float8_e4m3fn_x4", "uint8", "bfloat16", "float32", "int32", "uint16"
+PARTS = (((0, 256, ()), (256, C, ())), ((0, 256, ()), (256, C, ())),
+         ((0, 160, (0,)), (160, 288, (0,)), (288, C, (0,))), ((0, 192, (0,)), (192, C, ())))
+RX = 2
+G0 = 192
+
+SCRATCH = {"ps": ("psum", [128, 4096], F32)}
+for _n, _w in (("X", C), ("U", 128), ("UU", 256), ("V", 128), ("W", 512), ("E", 512), ("S", 256), ("T", 1536),
+               ("B", 128 * ROUNDS), ("L", 128 + K * ROUNDS), ("Z", C)):
+    SCRATCH["q" + _n] = ("sbuf", [128, _w], X4)
+    SCRATCH["s" + _n] = ("sbuf", [128, _w], U8)
+for _n, _w, _d in (("xt", 4 * C, BF), ("ut", 512, BF), ("vt", 512, BF), ("et", 2048, BF), ("st", 1024, BF),
+                   ("tt", 6144, BF), ("bt", 512, BF), ("zt", 4 * C, BF), ("fp", 4 * FW, BF), ("gp", 4 * FW, BF),
+                   ("gq", 4 * C, BF),
+                   ("iw", 768, F32), ("pi", 8, I32), ("cl", 10, F32), ("li", 40, I32), ("ul", 16, U16), ("xl", 24, U16),
+                   ("mi", 72, I32), ("mf", 72, F32), ("l4", 72, U16), ("l1", 72, U16), ("l3", 72, U16),
+                   ("md", 48, F32), ("dl", 48, U16), ("m2", 48, F32), ("e2", 32, F32),
+                   ("mk", C, BF), ("de", C, BF), ("dy", C, BF), ("dtr", 2 * C, F32), ("dd", 2 * C, BF), ("junk", 4224, BF),
+                   ("rs", 24, F32), ("rx", C, F32), ("rt", C, F32), ("yy", C, F32),
+                   ("da", 4 * C, BF), ("sa", 4 * C, BF), ("s1", 4 * C, BF), ("s2", 4 * C, BF), ("w3", C, F32),
+                   ("x3", 3 * C, F32), ("s3", 3 * C, F32), ("x4", 3 * C, BF), ("s4", 3 * C, F32),
+                   ("dmin", 3 * C, F32), ("dmax", 3 * C, F32), ("ey", C, F32), ("eo", K, F32), ("e3", C, F32),
+                   ("e4", C, F32), ("pl", 24, U16), ("ow", C, F32), ("ol", 6, U16), ("sm", 144, F32),
+                   ("ti", 48, I32), ("tl", 24, U16), ("otb", C, F32), ("yb", C, F32)):
+    SCRATCH[_n] = ("sbuf", [128, _w], _d)
+
+NDMA = 18
+SEMAPHORES = ["cV", "cA", "cP", "cG", "sent"] + ["arr%d" % n for n in range(ROUNDS)] + ["d%d" % n for n in range(NDMA)]
+
+
+def rank_program(g, core, T, topo):
+    rank = T.rank_of(core)
+    if rank is None:
+        return
+    A, F = AluOpType, ActivationFunctionType
+    queue = {"V": g.vector, "A": g.scalar, "P": g.tensor, "G": g, "S": g.sync}
+    ops = []
+
+    def v(name, a=0, b=None, s=1, p=None):
+        return (name, a, SCRATCH[name][1][1] if b is None else b, s, p)
+
+    def ap(r):
+        rows = slice(0, 128) if r[4] is None else slice(*r[4])
+        return T[r[0]][rows, r[1]:r[2]:r[3]] if r[3] != 1 else T[r[0]][rows, r[1]:r[2]]
+
+    def bank(k, n, a=0):
+        return v("ps", 512 * k + a, 512 * k + n)
+
+    def col(k):
+        return v("cl", k, k + 1)
+
+    def src(r):
+        if isinstance(r, list):
+            return ap(r[0]).indirect(ap(r[1]))
+        return ap(r) if isinstance(r, tuple) else r
+
+    def regs(*rs):
+        out = []
+        for r in rs:
+            if isinstance(r, list):
+                out += r
+            elif isinstance(r, tuple):
+                out.append(r)
+        return out
+
+    def op(q, f, reads, writes, kind="c", sem=None, count=0):
+        ops.append({"q": q, "f": f, "r": reads, "w": writes, "k": kind, "sem": sem, "n": count})
+
+    def ts(out, in0, s1, op0, s2=None, op1=None):
+        if op1 is None:
+            op("V", lambda: g.vector.tensor_scalar(ap(out), src(in0), src(s1), None, op0), regs(in0, s1), [out])
+        else:
+            op("V", lambda: g.vector.tensor_scalar(ap(out), src(in0), src(s1), src(s2), op0, op1), regs(in0, s1, s2), [out])
+
+    def tt(out, in0, in1, o):
+        op("V", lambda: g.vector.tensor_tensor(ap(out), src(in0), ap(in1), o), regs(in0, in1), [out])
+
+    def cp(out, in_):
+        op("V", lambda: g.vector.tensor_copy(ap(out), src(in_)), regs(in_), [out])
+
+    def fill(out, c):
+        op("V", lambda: g.vector.memset(ap(out), c), [], [out])
+
+    def scan(out, d0, d1, o):
+        op("V", lambda: g.vector.tensor_tensor_scan(ap(out), ap(d0), ap(d1), 0.0, A.add, o), [d0, d1], [out])
+
+    def turn(out, in_):
+        op("V", lambda: g.vector.transpose(ap(out), ap(in_)), [in_], [out])
+
+    def quant(n, a, b, in_):
+        q, s = v("q" + n, a, b), v("s" + n, a, b)
+        op("V", lambda: g.vector.quantize_mx(ap(q), ap(s), ap(in_)), [in_], [q, s])
+
+    def act(out, in_, scale=1.0, bias=None, accum=None, func=F.Identity):
+        if accum is not None:
+            op("A", lambda: g.scalar.activation(ap(out), src(in_), func, bias=bias, scale=scale, accum_out=ap(accum)),
+               regs(in_), [out, accum])
+        elif bias is not None:
+            op("A", lambda: g.scalar.activation(ap(out), src(in_), func, bias=src(bias), scale=scale), regs(in_, bias), [out])
+        elif scale != 1.0:
+            op("A", lambda: g.scalar.activation(ap(out), src(in_), F.Copy, scale=scale), regs(in_), [out])
+        else:
+            op("A", lambda: g.scalar.activation(ap(out), src(in_), F.Copy), regs(in_), [out])
+
+    def mm(k, w, wa, m, ma, n, start=True, stop=True):
+        r = [v("q" + w, wa, wa + 128), v("s" + w, wa, wa + 128), v("q" + m, ma, ma + n), v("s" + m, ma, ma + n)]
+        op("P", lambda: g.tensor.matmul_mx(ap(bank(k, n)), ap(r[0]), ap(r[1]), ap(r[2]), ap(r[3]), start, stop), r, [bank(k, n)])
+
+    def iota(out, pattern, base, cm):
+        if SCRATCH[out[0]][2] == I32:
+            op("G", lambda: g.iota(ap(out), pattern, base, cm), [], [out])
+        else:
+            op("G", lambda: g.iota(ap(out), pattern, base, cm, allow_small_or_imprecise_dtypes=True), [], [out])
+
+    ndma = [0]
+
+    def dma(q, out, in_, reads, writes):
+        op(q, lambda: queue[q].dma_start(out(), in_()), reads, writes, "dma", "d%d" % ndma[0], 16)
+        ndma[0] += 1
+
+    def codes(r):
+        return ap(r).bitcast(dt.uint8)
+
+    def lanes(a, b):
+        return topo.engines(a, b)[:8]
+
+    dest = T.cores[(rank - 1) % len(T.cores)]
+    origin = T.cores[(rank + 1) % len(T.cores)]
+    rid, pid, _ = topo.addr(dest)
+    emask = sum(1 << e for e in lanes(core, dest))
+
+    def send(n):
+        q, s = v("qB", 128 * n, 128 * n + K), v("sB", 128 * n, 128 * n + K)
+        lq, ls = v("qL", 128 + K * n, 128 + K * n + K), v("sL", 128 + K * n, 128 + K * n + K)
+        sem = T.sem["arr%d" % n]
+        op("G", lambda: g.remote_dma(codes(lq), codes(q), sem, T.sem.sent, pid, rid, emask), [q], [], "remote")
+        op("G", lambda: g.remote_dma(ap(ls), ap(s), sem, T.sem.sent, pid, rid, emask), [s], [], "remote")
+        op("X", None, [], [lq, ls], "dma", "arr%d" % n, 2 * len(lanes(origin, core)))
+
+    runs = ((0, H), (H, C))
+
+    for a, b in runs:
+        dma("S", lambda a=a, b=b: ap(v("xt", 4 * a, 4 * b)), lambda a=a, b=b: T.x[:, 4 * a:4 * b], [], [v("xt", 4 * a, 4 * b)])
+    dma("A", lambda: ap(v("ut")), lambda: T.u[:], [], [v("ut")])
+    dma("A", lambda: ap(v("mi")), lambda: T.mv[:], [], [v("mi")])
+    dma("S", lambda: codes(v("qW")), lambda: T.wc[:], [v("xt")], [v("qW")])
+    dma("S", lambda: ap(v("sW")), lambda: T.ws[:], [], [v("sW")])
+    dma("S", lambda: ap(v("vt")), lambda: T.v[:], [], [v("vt")])
+
+    iota(v("li", 0, 16), [[16, 2], [32, 4], [0, 2]], 0, 0)
+    iota(v("pi", 0, 1), [[0, 1]], 0, 1)
+    iota(v("iw", 0, 128), [[1, 128]], 0, 0)
+    iota(v("li", 16, 40), [[1, 12], [12, 2]], 0, 0)
+    holes = [v("tt", 3072 * h + 4 * a, 3072 * h + 4 * a + 384) for h in range(2) for a in (288, 384 + 160, 640 + 32)]
+    for r in holes[3:]:
+        iota(r, [[0, 384]], 0, 0)
+    iota(v("et"), [[0, 2048]], 0, 0)
+    for b in range(4):
+        e = v("et", 513 * b, 512 * b + 512, 4)
+        op("G", lambda e=e: g.affine_select(ap(e), ap(e), [[1, 128]], A.not_equal, 1.0, 0, -1), [e], [e])
+    iota(v("iw", 128, 768), [[1, 640]], 128, 0)
+    iota(v("da", 0, 4 * C, 4), [[0, C]], -16, 0)
+    iota(v("da", 1, 4 * C, 4), [[0, C]], 0, 0)
+    iota(v("da", 2, 4 * C, 4), [[0, C]], 0, 0)
+    iota(v("dmin", 0, 3 * C, 3), [[0, C]], FILL, 0)
+    iota(v("dmax", 0, 3 * C, 3), [[0, C]], -FILL, 0)
+
+    fill(v("st"), 0.0)
+    ts(v("pi", 1, 2), v("pi", 0, 1), 31, A.bitwise_and)
+    ts(v("pi", 2, 3), v("pi", 0, 1), 15, A.bitwise_and)
+    fill(v("bt"), 0.0)
+    cp(v("cl", 0, 3), v("pi", 0, 3))
+    cp(v("ul"), v("li", 0, 16))
+    ts(col(3), col(2), 1.0, A.add)
+    ts(v("mk", 0, 32), v("iw", 0, 32), col(1), A.is_gt, -TINY, A.mult)
+    ts(v("e2", 0, 16), v("iw", 0, 16), col(2), A.is_equal, BIG, A.mult)
+    ts(v("e2", 16, 32), v("iw", 0, 16), col(3), A.is_equal, -6 * U, A.mult)
+    ts(col(4), col(2), 14.5, A.is_lt, 6 * U, A.mult)
+    ts(col(8), col(2), 14.5, A.is_lt, 6.0, A.mult)
+    tt(v("de", 0, 16), v("e2", 0, 16), v("e2", 16, 32), A.add)
+    for name, w in (("mk", 32), ("de", 16)):
+        while w < C:
+            n = min(w, C - w)
+            act(v(name, w, w + n), v(name, 0, n))
+            w += n
+    act(v("dy"), v("de"), 1.0 / U)
+    for h in range(2):
+        for q in range(4):
+            a = 512 * h + 4 * (32 * q + 16 * h)
+            fill(v("st", a, a + 64, 1, (32 * q, 32 * q + 32)), STEP)
+    for r in holes[:3]:
+        fill(r, 0.0)
+    ts(col(5), col(8), -YB, A.add)
+    ts(col(6), col(8), 1.0 / STEP, A.mult, K - YB / STEP, A.add)
+    ts(col(7), col(8), -CUT, A.add)
+    quant("S", 0, 256, v("st"))
+    fill(v("rs"), 0.0)
+    quant("L", 0, 128, v("bt"))
+    cp(v("xl"), v("li", 16, 40))
+    quant("U", 0, 128, v("ut"))
+    op("V", lambda: g.vector.tensor_copy(ap(v("qUU")).bitcast(dt.uint32), ap(v("qU")).bitcast(dt.uint32).indirect(ap(v("ul")))),
+       [v("qU"), v("ul")], [v("qUU")])
+    act(v("sUU"), [v("sU"), v("ul")])
+    for b in range(3):
+        act(v("fp", FW * b, FW * b + C), v("xt", b, 4 * C, 4), 32.0)
+    for a, b in runs:
+        quant("X", a, b, v("xt", 4 * a, 4 * b))
+
+    def move_lists():
+        cp(v("mf"), v("mi"))
+        cp(v("l1"), v("mi"))
+        tt(v("md"), v("mf", 0, 48), v("mf", 24, 72), A.subtract)
+        ts(v("l4"), v("mi"), 4.0, A.mult, 3.0, A.add)
+        ts(v("dl"), v("md"), float(C), A.add)
+
+    def more_lists():
+        ts(v("l3"), v("mi"), 3.0, A.mult, 2.0, A.add)
+        ts(v("m2", 0, 24), v("mf", 48, 72), col(4), A.add, -1.125 * U, A.add)
+        ts(v("m2", 24, 48), v("mf", 48, 72), col(4), A.add)
+        quant("E", 0, 512, v("et"))
+
+    def plane(h, b):
+        if b == 0:
+            return v("tt", 3072 * h, 3072 * h + 4 * C, 4)
+        base, t = (0, 12 - b) if b > 8 else ((4 * 384, 8 - b) if b > 4 else (4 * 640, 4 - b))
+        a = 3072 * h + base + t
+        return v("tt", a, a + 4 * 32 * b - t, 4)
+
+    def last(name, n=C):
+        return v(name, 15, n, 16)
+
+    def sweep(win, lst, into, slots, parts, scale, bias, func, d0, out, o, between=None, after=None, mid=None):
+        def sides(a, b, k):
+            return v(into, slots * a + k, slots * b, slots), [win, v(lst, 24 * k + a // 16, 24 * k + b // 16)]
+        for i, (a, b, vk) in enumerate(parts):
+            for k in range(3):
+                if k not in vk:
+                    dst, wl = sides(a, b, k)
+                    act(dst, wl, scale, bias, None, func)
+            if i == 0 and mid is not None:
+                mid()
+        for k in range(3):
+            mine = [p for p in parts if k in p[2]]
+            if mine:
+                dst, wl = sides(mine[0][0], mine[-1][1], k)
+                if bias is None:
+                    cp(dst, wl)
+                else:
+                    ts(dst, wl, scale, A.mult, bias, A.add)
+        if between is not None:
+            between()
+        for a, b, vk in parts:
+            scan(v(out, slots * a, slots * b), v(d0, slots * a, slots * b), v(into, slots * a, slots * b), o)
+            if after is not None:
+                after(a, b)
+
+    def a_round(n):
+        mm(1, "UU", 0, "X", 0, H)
+        mm(0, "UU", 128, "X", 0, H)
+        mm(2, "UU", 128, "X", 0, H)
+        mm(4, "UU", 0, "X", 0, C)
+        mm(5, "UU", 128, "X", 0, C)
+        mm(7, "UU", 128, "X", H, C - H)
+        if n == 0:
+            move_lists()
+
+        def own(h, b):
+            return v("dtr", C * h + 32 * b, C * h + 32 * b + 1)
+
+        def pl(h, b):
+            ts(plane(h, b), bank(1 if h == 0 and 32 * b < H else 4 + h, 32 * b), own(h, b), A.is_lt)
+            a = 2112 * h + 16 * b * (b - 1)
+            act(v("junk", a, a + 32 * b), plane(h, b), -STEP, STEP, v("rs", 12 * h + b, 12 * h + b + 1))
+
+        def qa(h):
+            quant("T", 768 * h, 768 * h + C, v("tt", 3072 * h, 3072 * h + 4 * C))
+            mm(6, "S", 128 * h, "T", 768 * h, C, h == 0, h == 1)
+
+        def qbc(h):
+            quant("T", 768 * h + C, 768 * h + 768, v("tt", 3072 * h + 4 * C, 3072 * h + 3072))
+            mm(6, "S", 128 * h, "T", 768 * h + C, 256, False, False)
+            mm(6, "S", 128 * h, "T", 768 * h + 640, 128, False, False)
+
+        def inside(b):
+            act(v("dd", C + 32 * b, C + 32 * b + 32),
+                bank(2, 32 * b + 32, 32 * b) if 32 * b < H else bank(7, 32 * b + 32 - H, 32 * b - H), -1.0, own(1, b))
+
+        turn(v("dtr", 0, H), bank(1, H))
+        turn(v("dtr", C, C + H), bank(0, H))
+        for b in range(H // 32):
+            inside(b)
+        for b in (7, 6, 5):
+            pl(0, b)
+        turn(v("dtr", H, C), bank(4, C, H))
+        turn(v("dtr", C + H, 2 * C), bank(5, C, H))
+        for b in (4, 3, 2, 1):
+            pl(0, b)
+        for b in range(H // 32, 12):
+            inside(b)
+        tt(v("dd", 0, C), v("dtr", 0, C), bank(4, C), A.subtract)
+        for b in (11, 10):
+            pl(0, b)
+        tt(plane(0, 0), v("dd", 0, C), v("mk"), A.is_gt)
+        for b in (9, 8):
+            pl(0, b)
+        pl(1, 11)
+        qa(0)
+        for b in (10, 9):
+            pl(1, b)
+        qbc(0)
+        for b in range(8, 0, -1):
+            pl(1, b)
+            if b == RX:
+                act(v("rx", 32 * b, C), [v("rs"), v("xl", 2 * b, 24)], 1.0, YB)
+        tt(plane(1, 0), v("dd", C, 2 * C), v("mk"), A.is_gt)
+        qbc(1)
+        qa(1)
+        act(v("rx", 0, 32 * RX), [v("rs"), v("xl", 0, 2 * RX)], 1.0, YB)
+        turn(v("rt", 32 * RX, C), v("rx", 32 * RX, C))
+        turn(v("rt", 0, 32 * RX), v("rx", 0, 32 * RX))
+        if n == 0:
+            act(v("sa", 3, 4 * C, 4), v("bt", 0, C), 1.0, 0.5)
+        tt(v("yy"), bank(6, C), v("rt"), A.add)
+
+        def labels():
+            act(v("da", 3, 4 * C, 4), v("yy"), -1.0, CUT, None, F.Sign)
+
+        def places():
+            scan(v("ey"), v("dy"), v("yy"), A.min)
+            ts(v("pl"), last("ey"), col(5), A.add, 1.0 / STEP, A.mult)
+            op("V", lambda: g.vector.tensor_copy(ap(v("ow")).indirect(ap(v("pl"))), ap(v("iw", 0, C))),
+               [v("pl"), v("iw", 0, C)], [v("ow")])
+
+        def border():
+            scan(v("eo"), v("de", 0, K), v("ow", 0, K), A.min)
+            ts(v("sm", 0, 24), last("ey"), 1.0 / STEP, A.mult, col(6), A.add)
+            ts(v("ol"), last("eo", K), col(4), A.add)
+            ts(v("sm", 24, 48), last("ey"), col(7), A.add, -8 * U / (STEP / 2), A.mult)
+            for b in range(4):
+                ts(v("bt", b, 4 * K, 4), [v("fp", FW * b, FW * b + C), v("ol")], 1.0 / 32, A.mult)
+            tt(v("sm", 48, 72), v("sm", 0, 24), v("sm", 24, 48), A.max)
+            quant("B", 128 * n, 128 * n + 128, v("bt"))
+            send(n)
+            if n == 0:
+                more_lists()
+
+        def keys(a, b):
+            tt(v("w3", a, b), v("s2", 4 * a + 3, 4 * b, 4), v("yy", a, b), A.min)
+
+        def choice():
+            scan(v("e3"), v("de"), v("s3", 2, 3 * C, 3), A.min)
+            tt(v("sm", 72, 96), last("e3"), v("m2", 0, 24), A.add)
+            tt(v("sm", 96, 120), v("sm", 72, 96), v("sm", 48, 72), A.min)
+
+        def held(a, b):
+            scan(v("e4", a, b), v("de", a, b), v("s4", 3 * a + 2, 3 * b, 3), A.min)
+
+        sweep(v("yy"), "l1", "sa", 4, PARTS[0], 1.0, -CUT, F.Sign, "da", "s1", A.max, places, None, labels)
+        if n == 0:
+            ts(v("fp", FW * 3, FW * 3 + C), v("xt", 3, 4 * C, 4), 32.0, A.mult)
+        sweep(v("s1"), "l4", "sa", 4, PARTS[1], -1.0, 2.0, F.Sign, "da", "s2", A.max, border, keys)
+        if n == 0:
+            for k in (1, 2):
+                act(v("dmin", k, 3 * C, 3), [v("iw"), v("dl", 24 * k - 24, 24 * k)], 1.0, -C - PREF)
+        sweep(v("w3"), "l1", "x3", 3, PARTS[2], 2 * U, 2 * U, F.Identity, "dmin", "s3", A.min)
+        if n == 0:
+            for k in (1, 2):
+                act(v("dmax", k, 3 * C, 3), v("dmin", k, 3 * C, 3), 1.0, 2 * PREF)
+        for b in range(4):
+            mm(b, "E", 128 * b, "L", K + K * n, 128)
+        sweep(v("s3"), "l3", "x4", 3, PARTS[3], 1.0, None, F.Identity, "dmax", "s4", A.max, choice, held)
+        for b in range(4):
+            act(v("fp", FW * b + C, FW * b + FW), bank(b, 128, 32), 32.0)
+            act(v("gp", FW * b + C, FW * b + FW), bank(b, 128, 32), 0.5)
+        tt(v("sm", 120, 144), last("e4"), v("m2", 24, 48), A.add)
+        tt(v("ti", 0, 24), v("sm", 120, 144), v("sm", 96, 120), A.min)
+        ts(v("ti", 24, 48), v("ti", 0, 24), 511, A.bitwise_and)
+        cp(v("tl"), v("ti", 24, 48))
+
+        ts(v("gp", 0, G0), [v("fp", 0, FW), v("tl", 0, G0 // 16)], 1.0 / 64, A.mult)
+        act(v("gp", G0, C), [v("fp", 0, FW), v("tl", G0 // 16, 24)], 1.0 / 64)
+        for b in range(1, 4):
+            act(v("gp", FW * b, FW * b + C), [v("fp", FW * b, FW * b + FW), v("tl")], 1.0 / 64)
+        act(v("gq", 3 * C, 4 * C), v("gp", 3 * FW, 3 * FW + C))
+
+        def mean(b, lo, hi):
+            tt(v("zt", 4 * lo + b, 4 * hi, 4), [v("gp", FW * b, FW * b + FW), v("tl", lo // 16, hi // 16)],
+               v("gq", C * b + lo, C * b + hi), A.add)
+
+        for b in range(3):
+            cp(v("gq", C * b, C * b + C), v("gp", FW * b, FW * b + C))
+            mean(b, 0, C)
+        if n == ROUNDS - 1:
+            act(v("otb"), [v("iw"), v("tl")])
+            dma("S", lambda: T.ot[:], lambda: ap(v("otb", 0, C, 1, (0, 128, 16))), [v("otb")], [])
+
+        for i, (lo, hi) in enumerate(runs):
+            mean(3, lo, hi)
+            quant("Z", lo, hi, v("zt", 4 * lo, 4 * hi))
+            for b in range(4):
+                mm(4 * i + b, "W", 128 * b, "Z", lo, hi - lo)
+        if n == 0:
+            quant("V", 0, 128, v("vt"))
+        for i, (lo, hi) in enumerate(runs):
+            for b in range(4):
+                f = v("fp", FW * b + lo, FW * b + hi)
+                tt(f, bank(4 * i + b, hi - lo), f, A.add)
+                if b < 3 - i:
+                    act(v("xt", 4 * lo + b, 4 * hi, 4), f, 1.0 / 32)
+        ts(v("xt", 3, 4 * H, 4), v("fp", FW * 3, FW * 3 + H), 1.0 / 32, A.mult)
+        lo, hi = runs[1]
+        ts(v("xt", 4 * lo + 2, 4 * hi, 4), v("fp", FW * 2 + lo, FW * 2 + hi), 1.0 / 32, A.mult)
+        quant("X", 0, H, v("xt", 0, 4 * H))
+        ts(v("xt", 4 * lo + 3, 4 * hi, 4), v("fp", FW * 3 + lo, FW * 3 + hi), 1.0 / 32, A.mult)
+        quant("X", H, C, v("xt", 4 * H, 4 * C))
+
+    for n in range(ROUNDS):
+        a_round(n)
+
+    for i, (lo, hi) in enumerate(runs):
+        mm(i, "V", 0, "X", lo, hi - lo)
+        dma("SA"[i], lambda lo=lo, hi=hi: T.oc[:, 4 * lo:4 * hi], lambda lo=lo, hi=hi: codes(v("qX", lo, hi)), [v("qX", lo, hi)], [])
+    for k in range(4):
+        dma("SA"[k // 2], lambda k=k: T.osc[4 * k:4 * k + 4, :], lambda k=k: ap(v("sX", 0, C, 1, (32 * k, 32 * k + 4))), [v("sX")], [])
+    for i, (lo, hi) in enumerate(runs):
+        cp(v("yb", lo, hi), bank(i, hi - lo))
+        dma("AS"[i], lambda lo=lo, hi=hi: T.y[:, lo:hi], lambda lo=lo, hi=hi: ap(v("yb", lo, hi)), [v("yb", lo, hi)], [])
+
+    names = "VAPGSX"
+    wrote = {b: np.full(s[1][1], -1) for b, s in SCRATCH.items()}
+    read = {b: {q: np.full(s[1][1], -1) for q in names} for b, s in SCRATCH.items()}
+    known = {q: {} for q in names}
+    done, waits, waited = [], [], set()
+
+    def cols(r):
+        if r[0] == "ps":
+            return slice(r[1] // 512 * 512, r[1] // 512 * 512 + 512)
+        return slice(r[1], r[2], r[3])
+
+    def source(d):
+        return ops[d]["q"] if ops[d]["k"] == "c" else ops[d]["sem"]
+
+    for i, o in enumerate(ops):
+        q, deps, soft = o["q"], set(), set()
+        for r in o["r"]:
+            deps.update(int(d) for d in np.unique(wrote[r[0]][cols(r)]))
+            if r[0] == "ps":
+                for e in names:
+                    if e != q:
+                        deps.add(int(read["ps"][e][cols(r)].max()))
+        for r in o["w"]:
+            soft.update(int(d) for d in np.unique(wrote[r[0]][cols(r)]))
+            for e in names:
+                soft.add(int(read[r[0]][e][cols(r)].max()))
+        for d in soft:
+            if d >= 0 and (ops[d]["q"] != q or q != "P"):
+                deps.add(d)
+        mine = []
+        for d in sorted(deps, reverse=True):
+            if d >= 0 and q != "X" and known[q].get(source(d), -1) < d:
+                mine.append(d)
+                waited.add(d)
+                for s, w in done[d].items():
+                    known[q][s] = max(known[q].get(s, -1), w)
+        waits.append(mine)
+        done.append(dict(known[q]))
+        if o["k"] != "remote":
+            done[i][source(i)] = i
+        if o["k"] == "c":
+            for r in o["r"]:
+                read[r[0]][q][cols(r)] = i
+        for r in o["w"]:
+            wrote[r[0]][cols(r)] = i
+
+    count, total = {}, {q: 0 for q in names}
+    for i, o in enumerate(ops):
+        if o["k"] == "c" and i in waited:
+            total[o["q"]] += 1
+            count[i] = total[o["q"]]
+    for i, o in enumerate(ops):
+        for d in waits[i]:
+            if ops[d]["k"] == "c":
+                queue[o["q"]].wait_ge(T.sem["c" + ops[d]["q"]], count[d])
+            else:
+                queue[o["q"]].wait_ge(T.sem[ops[d]["sem"]], ops[d]["n"])
+        if o["q"] == "X":
+            continue
+        ins = o["f"]()
+        if o["k"] == "dma":
+            ins.then_inc(T.sem[o["sem"]], 16)
+        elif i in waited:
+            ins.then_inc(T.sem["c" + o["q"]], 1)
+    g.wait_ge(T.sem.sent, 2 * len(lanes(core, dest)) * ROUNDS)
+    for i, o in enumerate(ops):
+        if o["k"] == "dma" and i not in waited:
+            queue[o["q"]].wait_ge(T.sem[o["sem"]], o["n"])

@@ -15,8 +15,7 @@ TINY = 2.0 ** -120
 X4, U8, BF, F32, I32, U16 = "float8_e4m3fn_x4", "uint8", "bfloat16", "float32", "int32", "uint16"
 PARTS = (((0, 256, ()), (256, C, ())), ((0, 256, ()), (256, C, ())),
          ((0, 160, (0,)), (160, 288, (0,)), (288, C, (0,))), ((0, 192, (0,)), (192, C, ())))
-RX = 2
-G0 = 192
+NB = 4
 
 SCRATCH = {"ps": ("psum", [128, 4096], F32)}
 for _n, _w in (("X", C), ("U", 128), ("UU", 256), ("V", 128), ("W", 512), ("E", 512), ("S", 256), ("T", 1536),
@@ -274,7 +273,6 @@ def rank_program(g, core, T, topo):
         mm(2, "UU", 128, "X", 0, H)
         mm(4, "UU", 0, "X", 0, C)
         mm(5, "UU", 128, "X", 0, C)
-        mm(7, "UU", 128, "X", H, C - H)
         if n == 0:
             move_lists()
 
@@ -295,43 +293,38 @@ def rank_program(g, core, T, topo):
             mm(6, "S", 128 * h, "T", 768 * h + C, 256, False, False)
             mm(6, "S", 128 * h, "T", 768 * h + 640, 128, False, False)
 
-        def inside(b):
-            act(v("dd", C + 32 * b, C + 32 * b + 32),
-                bank(2, 32 * b + 32, 32 * b) if 32 * b < H else bank(7, 32 * b + 32 - H, 32 * b - H), -1.0, own(1, b))
+        def inside(h, a):
+            tt(v("dd", C * h + a, C * h + C), v("dtr", C * h + a, C * h + C), bank(4 + h, C, a), A.subtract)
+
+        def wins(h):
+            tt(plane(h, 0), v("dd", C * h, C * h + C), v("mk"), A.is_gt)
 
         turn(v("dtr", 0, H), bank(1, H))
         turn(v("dtr", C, C + H), bank(0, H))
-        for b in range(H // 32):
-            inside(b)
+        for b in range(NB):
+            act(v("dd", C + 32 * b, C + 32 * b + 32), bank(2, 32 * b + 32, 32 * b), -1.0, own(1, b))
         for b in (7, 6, 5):
             pl(0, b)
         turn(v("dtr", H, C), bank(4, C, H))
         turn(v("dtr", C + H, 2 * C), bank(5, C, H))
-        for b in (4, 3, 2, 1):
+        for b in (4, 3, 2, 1, 11, 10, 9, 8):
             pl(0, b)
-        for b in range(H // 32, 12):
-            inside(b)
-        tt(v("dd", 0, C), v("dtr", 0, C), bank(4, C), A.subtract)
+        inside(0, 0)
         for b in (11, 10):
-            pl(0, b)
-        tt(plane(0, 0), v("dd", 0, C), v("mk"), A.is_gt)
-        for b in (9, 8):
-            pl(0, b)
-        pl(1, 11)
+            pl(1, b)
+        wins(0)
+        for b in (9, 8, 7):
+            pl(1, b)
         qa(0)
-        for b in (10, 9):
+        for b in range(6, 0, -1):
             pl(1, b)
+        act(v("rx"), [v("rs"), v("xl")], 1.0, YB)
+        inside(1, 32 * NB)
         qbc(0)
-        for b in range(8, 0, -1):
-            pl(1, b)
-            if b == RX:
-                act(v("rx", 32 * b, C), [v("rs"), v("xl", 2 * b, 24)], 1.0, YB)
-        tt(plane(1, 0), v("dd", C, 2 * C), v("mk"), A.is_gt)
+        wins(1)
         qbc(1)
         qa(1)
-        act(v("rx", 0, 32 * RX), [v("rs"), v("xl", 0, 2 * RX)], 1.0, YB)
-        turn(v("rt", 32 * RX, C), v("rx", 32 * RX, C))
-        turn(v("rt", 0, 32 * RX), v("rx", 0, 32 * RX))
+        turn(v("rt"), v("rx"))
         if n == 0:
             act(v("sa", 3, 4 * C, 4), v("bt", 0, C), 1.0, 0.5)
         tt(v("yy"), bank(6, C), v("rt"), A.add)
@@ -361,18 +354,39 @@ def rank_program(g, core, T, topo):
         def keys(a, b):
             tt(v("w3", a, b), v("s2", 4 * a + 3, 4 * b, 4), v("yy", a, b), A.min)
 
+        def keys_after(a, b):
+            if a == 0:
+                keys(0, 128)
+            else:
+                keys(128, a)
+                keys(a, b)
+
         def choice():
             scan(v("e3"), v("de"), v("s3", 2, 3 * C, 3), A.min)
-            tt(v("sm", 72, 96), last("e3"), v("m2", 0, 24), A.add)
-            tt(v("sm", 96, 120), v("sm", 72, 96), v("sm", 48, 72), A.min)
+
+        def reply(a, b):
+            i, j = a // 16, b // 16
+            return [lambda: scan(v("e4", a, b), v("de", a, b), v("s4", 3 * a + 2, 3 * b, 3), A.min),
+                    lambda: tt(v("sm", 120 + i, 120 + j), v("e4", a + 15, b, 16), v("m2", 24 + i, 24 + j), A.add),
+                    lambda: tt(v("ti", i, j), v("sm", 120 + i, 120 + j), v("sm", 96 + i, 96 + j), A.min),
+                    lambda: ts(v("ti", 24 + i, 24 + j), v("ti", i, j), 511, A.bitwise_and),
+                    lambda: cp(v("tl", i, j), v("ti", 24 + i, 24 + j))]
 
         def held(a, b):
-            scan(v("e4", a, b), v("de", a, b), v("s4", 3 * a + 2, 3 * b, 3), A.min)
+            if a == 0:
+                tt(v("sm", 72, 96), last("e3"), v("m2", 0, 24), A.add)
+                reply(a, b)[0]()
+                tt(v("sm", 96, 120), v("sm", 72, 96), v("sm", 48, 72), A.min)
+                reply(a, b)[1]()
+            else:
+                first, second = reply(0, a), reply(a, b)
+                for step in (first[2], second[0], first[3], second[1], first[4], second[2], second[3], second[4]):
+                    step()
 
         sweep(v("yy"), "l1", "sa", 4, PARTS[0], 1.0, -CUT, F.Sign, "da", "s1", A.max, places, None, labels)
         if n == 0:
             ts(v("fp", FW * 3, FW * 3 + C), v("xt", 3, 4 * C, 4), 32.0, A.mult)
-        sweep(v("s1"), "l4", "sa", 4, PARTS[1], -1.0, 2.0, F.Sign, "da", "s2", A.max, border, keys)
+        sweep(v("s1"), "l4", "sa", 4, PARTS[1], -1.0, 2.0, F.Sign, "da", "s2", A.max, border, keys_after)
         if n == 0:
             for k in (1, 2):
                 act(v("dmin", k, 3 * C, 3), [v("iw"), v("dl", 24 * k - 24, 24 * k)], 1.0, -C - PREF)
@@ -386,24 +400,32 @@ def rank_program(g, core, T, topo):
         for b in range(4):
             act(v("fp", FW * b + C, FW * b + FW), bank(b, 128, 32), 32.0)
             act(v("gp", FW * b + C, FW * b + FW), bank(b, 128, 32), 0.5)
-        tt(v("sm", 120, 144), last("e4"), v("m2", 24, 48), A.add)
-        tt(v("ti", 0, 24), v("sm", 120, 144), v("sm", 96, 120), A.min)
-        ts(v("ti", 24, 48), v("ti", 0, 24), 511, A.bitwise_and)
-        cp(v("tl"), v("ti", 24, 48))
 
-        ts(v("gp", 0, G0), [v("fp", 0, FW), v("tl", 0, G0 // 16)], 1.0 / 64, A.mult)
-        act(v("gp", G0, C), [v("fp", 0, FW), v("tl", G0 // 16, 24)], 1.0 / 64)
-        for b in range(1, 4):
-            act(v("gp", FW * b, FW * b + C), [v("fp", FW * b, FW * b + FW), v("tl")], 1.0 / 64)
+        def half(b, lo, hi):
+            return v("gp", FW * b + lo, FW * b + hi), [v("fp", FW * b, FW * b + FW), v("tl", lo // 16, hi // 16)]
+
+        cut = PARTS[3][0][1]
+        for b in range(2):
+            act(*half(b, 0, cut), 1.0 / 64)
+        ts(*half(0, cut, C), 1.0 / 64, A.mult)
+        act(*half(1, cut, C), 1.0 / 64)
+        for b in range(2, 4):
+            act(*half(b, 0, C), 1.0 / 64)
         act(v("gq", 3 * C, 4 * C), v("gp", 3 * FW, 3 * FW + C))
 
         def mean(b, lo, hi):
             tt(v("zt", 4 * lo + b, 4 * hi, 4), [v("gp", FW * b, FW * b + FW), v("tl", lo // 16, hi // 16)],
                v("gq", C * b + lo, C * b + hi), A.add)
 
-        for b in range(3):
+        def twin(b):
             cp(v("gq", C * b, C * b + C), v("gp", FW * b, FW * b + C))
-            mean(b, 0, C)
+
+        twin(0)
+        twin(1)
+        mean(0, 0, C)
+        twin(2)
+        mean(1, 0, C)
+        mean(2, 0, C)
         if n == ROUNDS - 1:
             act(v("otb"), [v("iw"), v("tl")])
             dma("S", lambda: T.ot[:], lambda: ap(v("otb", 0, C, 1, (0, 128, 16))), [v("otb")], [])
@@ -415,17 +437,22 @@ def rank_program(g, core, T, topo):
                 mm(4 * i + b, "W", 128 * b, "Z", lo, hi - lo)
         if n == 0:
             quant("V", 0, 128, v("vt"))
-        for i, (lo, hi) in enumerate(runs):
-            for b in range(4):
-                f = v("fp", FW * b + lo, FW * b + hi)
-                tt(f, bank(4 * i + b, hi - lo), f, A.add)
-                if b < 3 - i:
-                    act(v("xt", 4 * lo + b, 4 * hi, 4), f, 1.0 / 32)
-        ts(v("xt", 3, 4 * H, 4), v("fp", FW * 3, FW * 3 + H), 1.0 / 32, A.mult)
-        lo, hi = runs[1]
-        ts(v("xt", 4 * lo + 2, 4 * hi, 4), v("fp", FW * 2 + lo, FW * 2 + hi), 1.0 / 32, A.mult)
+
+        def add(i, b):
+            lo, hi = runs[i]
+            f = v("fp", FW * b + lo, FW * b + hi)
+            tt(f, bank(4 * i + b, hi - lo), f, A.add)
+            return v("xt", 4 * lo + b, 4 * hi, 4), f
+
+        for b in range(3):
+            act(*add(0, b), 1.0 / 32)
+        late = [add(0, 3), add(1, 0)]
+        ts(*late[0], 1.0 / 32, A.mult)
+        act(*late[1], 1.0 / 32)
+        late = [add(1, b) for b in range(1, 4)]
         quant("X", 0, H, v("xt", 0, 4 * H))
-        ts(v("xt", 4 * lo + 3, 4 * hi, 4), v("fp", FW * 3 + lo, FW * 3 + hi), 1.0 / 32, A.mult)
+        for r in late:
+            ts(*r, 1.0 / 32, A.mult)
         quant("X", H, C, v("xt", 4 * H, 4 * C))
 
     for n in range(ROUNDS):

@@ -4,41 +4,59 @@ from concourse.mybir import dt, AluOpType, ActivationFunctionType
 C, K, ROUNDS = 384, 96, 3
 FW = C + K
 H = 256
-STEP = 2.0 ** -10
-YB = 1.625
-CUT = YB + (C - K - 0.5) * STEP
+NBLK = C // 16
+RW = 192
+STEP = 2.0 ** -9
+MID = 192
 U = float(2 ** 21)
+LOW = 3.0
+SHIFT = 19.0 / 32
 PREF = 512.0
 BIG = float(2 ** 26)
+FAR = 2.0 ** 90
 FILL = 15000000
 TINY = 2.0 ** -120
 X4, U8, BF, F32, I32, U16 = "float8_e4m3fn_x4", "uint8", "bfloat16", "float32", "int32", "uint16"
-PARTS = (((0, 256, ()), (256, C, ())), ((0, 256, ()), (256, C, ())),
-         ((0, 160, (0,)), (160, 288, (0,)), (288, C, (0,))), ((0, 192, (0,)), (192, C, ())))
-NB = 4
+TILES = ((0, 384), (384, 320), (704, 256), (960, 192), (1152, 128), (1280, 128))
+THEIRS = (15, 14, 20, 19, 18, 17, 16, 13)
+MINE = (23, 22, 21, 2, (0, 0), 3, 4, 5, 6, 7, 8, 9, 10, 11, (4, 5), 12)
+CLOSE = ((3, 3), (1, 1), (2, 2))
+PARTS = (((0, 256, ()), (256, C, (0, 3))), ((0, 224, (0,)), (224, C, (0, 1))),
+         ((0, 160, (0,)), (160, 288, (0,)), (288, C, (0,))), ((0, 256, (0,)), (256, C, ())))
+REPLY = ((0, 256), (256, C))
+SPLIT = 1
+MEANS = (((0, C),), ((0, C),), ((0, H), (H, C)))
+OWN = ()
+BV = 2
+WAKE, TRIP, TURNS = 240, 1500, 2
 
 SCRATCH = {"ps": ("psum", [128, 4096], F32)}
-for _n, _w in (("X", C), ("U", 128), ("UU", 256), ("V", 128), ("W", 512), ("E", 512), ("S", 256), ("T", 1536),
+for _n, _w in (("X", C), ("U", 128), ("UU", 128), ("V", 128), ("W", 512), ("E", 512), ("S", 256), ("T", 1408),
                ("B", 128 * ROUNDS), ("L", 128 + K * ROUNDS), ("Z", C)):
     SCRATCH["q" + _n] = ("sbuf", [128, _w], X4)
     SCRATCH["s" + _n] = ("sbuf", [128, _w], U8)
-for _n, _w, _d in (("xt", 4 * C, BF), ("ut", 512, BF), ("vt", 512, BF), ("et", 2048, BF), ("st", 1024, BF),
-                   ("tt", 6144, BF), ("bt", 512, BF), ("zt", 4 * C, BF), ("fp", 4 * FW, BF), ("gp", 4 * FW, BF),
-                   ("gq", 4 * C, BF),
-                   ("iw", 768, F32), ("pi", 8, I32), ("cl", 10, F32), ("li", 40, I32), ("ul", 16, U16), ("xl", 24, U16),
-                   ("mi", 72, I32), ("mf", 72, F32), ("l4", 72, U16), ("l1", 72, U16), ("l3", 72, U16),
-                   ("md", 48, F32), ("dl", 48, U16), ("m2", 48, F32), ("e2", 32, F32),
-                   ("mk", C, BF), ("de", C, BF), ("dy", C, BF), ("dtr", 2 * C, F32), ("dd", 2 * C, BF), ("junk", 4224, BF),
-                   ("rs", 24, F32), ("rx", C, F32), ("rt", C, F32), ("yy", C, F32),
-                   ("da", 4 * C, BF), ("sa", 4 * C, BF), ("s1", 4 * C, BF), ("s2", 4 * C, BF), ("w3", C, F32),
+for _n, _w, _d in (("xt", 4 * C, BF), ("ut", 512, BF), ("vt", 512, BF), ("et", 2048, BF), ("st", 1024, BF), ("gi", 512, BF),
+                   ("tt", 4 * 1408, BF), ("bt", 512, BF), ("zt", 4 * C, BF), ("fp", 4 * FW, BF), ("fq", 4 * C, BF),
+                   ("hp", 4 * FW, BF),
+                   ("iw", 768, F32), ("pi", 8, I32), ("cl", 16, F32), ("li", 56, I32), ("ul", 8, U16), ("rl", 24, U16),
+                   ("lo", 24, U16), ("mi", 72, I32), ("mj", 216, I32), ("mf", 72, F32), ("lk", 72, U16), ("l4", 72, U16),
+                   ("l3", 72, U16), ("md", 72, F32), ("dl", 72, U16), ("m2", 72, F32), ("e2", 64, F32), ("pat", 48, F32),
+                   ("mk", C, BF), ("hd", C, BF), ("de", C, BF), ("dy", C, BF), ("sg", 2 * C, BF), ("sp", 2 * C, BF),
+                   ("sq", 2 * C, BF), ("kw", 2 * C, BF), ("ms", C, F32), ("hh", C, F32), ("sb", C, BF),
+                   ("dd", 16 * 276, BF), ("rj", RW * NBLK, F32), ("ec", C, F32), ("pk", 168, F32),
+                   ("da", 4 * C, BF), ("sa", 4 * C, BF), ("s1", 4 * C, BF), ("s2", 4 * C, BF),
                    ("x3", 3 * C, F32), ("s3", 3 * C, F32), ("x4", 3 * C, BF), ("s4", 3 * C, F32),
-                   ("dmin", 3 * C, F32), ("dmax", 3 * C, F32), ("ey", C, F32), ("eo", K, F32), ("e3", C, F32),
+                   ("dmin", 3 * C, F32), ("dmax", 3 * C, F32), ("eo", K, F32), ("e3", C, F32),
                    ("e4", C, F32), ("pl", 24, U16), ("ow", C, F32), ("ol", 6, U16), ("sm", 144, F32),
                    ("ti", 48, I32), ("tl", 24, U16), ("otb", C, F32), ("yb", C, F32)):
     SCRATCH[_n] = ("sbuf", [128, _w], _d)
 
-NDMA = 18
+NDMA = 30
 SEMAPHORES = ["cV", "cA", "cP", "cG", "sent"] + ["arr%d" % n for n in range(ROUNDS)] + ["d%d" % n for n in range(NDMA)]
+
+
+def above(b):
+    return sum(1 for x in range(b + 1, max(THEIRS)) if x not in THEIRS) - max(0, b - max(THEIRS))
 
 
 def rank_program(g, core, T, topo):
@@ -76,8 +94,10 @@ def rank_program(g, core, T, topo):
                 out.append(r)
         return out
 
-    def op(q, f, reads, writes, kind="c", sem=None, count=0):
-        ops.append({"q": q, "f": f, "r": reads, "w": writes, "k": kind, "sem": sem, "n": count})
+    def op(q, f, reads, writes, kind="c", sem=None, count=0, scatter=0):
+        ops.append({"q": q, "f": f, "r": reads, "w": writes, "k": kind, "sem": sem, "n": count, "s": scatter, "row": row[0]})
+
+    row = [None]
 
     def ts(out, in0, s1, op0, s2=None, op1=None):
         if op1 is None:
@@ -94,8 +114,8 @@ def rank_program(g, core, T, topo):
     def fill(out, c):
         op("V", lambda: g.vector.memset(ap(out), c), [], [out])
 
-    def scan(out, d0, d1, o):
-        op("V", lambda: g.vector.tensor_tensor_scan(ap(out), ap(d0), ap(d1), 0.0, A.add, o), [d0, d1], [out])
+    def scan(out, d0, d1, o, o0=A.add, first=0.0):
+        op("V", lambda: g.vector.tensor_tensor_scan(ap(out), ap(d0), ap(d1), first, o0, o), [d0, d1], [out])
 
     def turn(out, in_):
         op("V", lambda: g.vector.transpose(ap(out), ap(in_)), [in_], [out])
@@ -160,283 +180,266 @@ def rank_program(g, core, T, topo):
     dma("S", lambda: ap(v("sW")), lambda: T.ws[:], [], [v("sW")])
     dma("S", lambda: ap(v("vt")), lambda: T.v[:], [], [v("vt")])
 
-    iota(v("li", 0, 16), [[16, 2], [32, 4], [0, 2]], 0, 0)
     iota(v("pi", 0, 1), [[0, 1]], 0, 1)
-    iota(v("iw", 0, 128), [[1, 128]], 0, 0)
-    iota(v("li", 16, 40), [[1, 12], [12, 2]], 0, 0)
-    holes = [v("tt", 3072 * h + 4 * a, 3072 * h + 4 * a + 384) for h in range(2) for a in (288, 384 + 160, 640 + 32)]
-    for r in holes[3:]:
-        iota(r, [[0, 384]], 0, 0)
-    iota(v("et"), [[0, 2048]], 0, 0)
-    for b in range(4):
-        e = v("et", 513 * b, 512 * b + 512, 4)
-        op("G", lambda e=e: g.affine_select(ap(e), ap(e), [[1, 128]], A.not_equal, 1.0, 0, -1), [e], [e])
-    iota(v("iw", 128, 768), [[1, 640]], 128, 0)
+    iota(v("iw", 0, 16), [[1, 16]], 0, 0)
+    iota(v("li", 0, 8), [[16, 8]], 0, 0)
+    iota(v("li", 8, 32), [[0, NBLK]], 0, 1)
+    iota(v("li", 32, 56), [[32, NBLK]], 0, 0)
+    iota(v("gi"), [[1, 8], [0, 64]], 0, 0)
+    iota(v("sg"), [[0, 2 * C]], 1, 0)
+    iota(v("sg", 0, 2 * C, 32), [[0, NBLK]], 0, 0)
+    iota(v("sp"), [[0, 2 * C]], 0, 0)
+    iota(v("iw", 16, 768), [[1, 752]], 16, 0)
     iota(v("da", 0, 4 * C, 4), [[0, C]], -16, 0)
-    iota(v("da", 1, 4 * C, 4), [[0, C]], 0, 0)
-    iota(v("da", 2, 4 * C, 4), [[0, C]], 0, 0)
-    iota(v("dmin", 0, 3 * C, 3), [[0, C]], FILL, 0)
-    iota(v("dmax", 0, 3 * C, 3), [[0, C]], -FILL, 0)
+    iota(v("da", 1, 4 * C, 4), [[0, C]], 16, 0)
+    iota(v("da", 2, 4 * C, 4), [[0, C]], 16, 0)
+    iota(v("sa", 3, 4 * C, 4), [[0, C]], -2, 0)
 
-    fill(v("st"), 0.0)
+    def late_constants():
+        for b in range(4):
+            e = v("et", 513 * b, 512 * b + 512, 4)
+            op("G", lambda e=e: g.affine_select(ap(e), ap(e), [[1, 128]], A.not_equal, 1.0, 0, -1), [e], [e])
+        iota(v("dmin", 0, 3 * C, 3), [[0, C]], FILL, 0)
+
+    fill(v("et"), 0.0)
     ts(v("pi", 1, 2), v("pi", 0, 1), 31, A.bitwise_and)
     ts(v("pi", 2, 3), v("pi", 0, 1), 15, A.bitwise_and)
+    ts(v("pi", 3, 4), v("pi", 0, 1), 16, A.bitwise_and)
+    ts(v("pi", 4, 5), v("pi", 0, 1), 4, A.arith_shift_right)
     fill(v("bt"), 0.0)
-    cp(v("cl", 0, 3), v("pi", 0, 3))
-    cp(v("ul"), v("li", 0, 16))
-    ts(col(3), col(2), 1.0, A.add)
-    ts(v("mk", 0, 32), v("iw", 0, 32), col(1), A.is_gt, -TINY, A.mult)
-    ts(v("e2", 0, 16), v("iw", 0, 16), col(2), A.is_equal, BIG, A.mult)
-    ts(v("e2", 16, 32), v("iw", 0, 16), col(3), A.is_equal, -6 * U, A.mult)
-    ts(col(4), col(2), 14.5, A.is_lt, 6 * U, A.mult)
-    ts(col(8), col(2), 14.5, A.is_lt, 6.0, A.mult)
-    tt(v("de", 0, 16), v("e2", 0, 16), v("e2", 16, 32), A.add)
-    for name, w in (("mk", 32), ("de", 16)):
-        while w < C:
-            n = min(w, C - w)
-            act(v(name, w, w + n), v(name, 0, n))
-            w += n
-    act(v("dy"), v("de"), 1.0 / U)
-    for h in range(2):
-        for q in range(4):
-            a = 512 * h + 4 * (32 * q + 16 * h)
-            fill(v("st", a, a + 64, 1, (32 * q, 32 * q + 32)), STEP)
-    for r in holes[:3]:
-        fill(r, 0.0)
-    ts(col(5), col(8), -YB, A.add)
-    ts(col(6), col(8), 1.0 / STEP, A.mult, K - YB / STEP, A.add)
-    ts(col(7), col(8), -CUT, A.add)
-    quant("S", 0, 256, v("st"))
-    fill(v("rs"), 0.0)
+    cp(v("cl", 0, 5), v("pi", 0, 5))
+    cp(v("ul"), v("li", 0, 8))
+    ts(v("li", 8, 32), v("li", 8, 32), 15, A.bitwise_and)
+    ts(col(5), col(2), 1.0, A.add)
+    ts(v("e2", 0, 16), v("iw", 0, 16), col(2), A.is_equal)
+    ts(col(6), col(2), 14.5, A.is_lt, LOW * U, A.mult)
+    cp(v("rl"), v("li", 8, 32))
+    ts(v("e2", 16, 32), v("iw", 0, 16), col(5), A.is_equal, -LOW * U, A.mult)
+    ts(v("pat", 0, 16), v("e2", 0, 16), 2 * FAR, A.mult, -FAR, A.add)
+    ts(v("pat", 16, 32), v("e2", 0, 16), -4 * FAR, A.mult)
+    ts(v("e2", 32, 48), v("e2", 0, 16), BIG, A.mult)
+    ts(col(7), col(6), 1.0 / U, A.mult, (8 * max(THEIRS) - MID) * STEP, A.add)
+    ts(v("pat", 16, 17), v("e2", 0, 1), -6 * FAR, A.mult, 2 * FAR, A.add)
+    tt(v("pat", 32, 48), v("e2", 32, 48), v("e2", 16, 32), A.add)
+    ts(col(8), col(2), STEP, A.mult, col(7), A.add)
+    for k, name in enumerate(("mk", "hd", "de")):
+        act(v(name), [v("pat", 16 * k, 16 * k + 16), v("rl")])
+    for a, w in TILES[:-1]:
+        fill(v("tt", 4 * (a + w - 48), 4 * (a + w)), 0.0)
+    fill(v("tt", 4 * TILES[-1][0], 4 * sum(TILES[-1])), 0.0)
+    fill(v("rj", RW - 1, RW), 16.0 * above(0))
     quant("L", 0, 128, v("bt"))
-    cp(v("xl"), v("li", 16, 40))
+    ts(v("lo"), v("li", 32, 56), col(1), A.add)
     quant("U", 0, 128, v("ut"))
+    for h in range(2):
+        ts(v("st", 512 * h, 512 * h + 512), v("gi"), col(4), A.is_equal, STEP / 2, A.mult)
     op("V", lambda: g.vector.tensor_copy(ap(v("qUU")).bitcast(dt.uint32), ap(v("qU")).bitcast(dt.uint32).indirect(ap(v("ul")))),
        [v("qU"), v("ul")], [v("qUU")])
     act(v("sUU"), [v("sU"), v("ul")])
-    for b in range(3):
-        act(v("fp", FW * b, FW * b + C), v("xt", b, 4 * C, 4), 32.0)
+    ts(v("st", 0, 512, 4), v("st", 0, 512, 4), -2.0, A.mult)
     for a, b in runs:
         quant("X", a, b, v("xt", 4 * a, 4 * b))
+    quant("S", 0, 256, v("st"))
+
+    def twin(b):
+        dma("S", lambda: ap(v("fq", C * b, C * b + C)), lambda: ap(v("fp", FW * b, FW * b + C)),
+            [v("fp", FW * b, FW * b + C)], [v("fq", C * b, C * b + C)])
+
+    def planes():
+        act(v("dy"), v("de"), 1.0 / U)
+        for b in range(4):
+            act(v("fp", FW * b, FW * b + C), v("xt", b, 4 * C, 4), 32.0)
+            if b < 3:
+                twin(b)
 
     def move_lists():
+        ts(v("mj", 0, 72), v("mi"), 4, A.arith_shift_right)
         cp(v("mf"), v("mi"))
-        cp(v("l1"), v("mi"))
-        tt(v("md"), v("mf", 0, 48), v("mf", 24, 72), A.subtract)
+        ts(v("mj", 72, 144), v("mj", 0, 72), 16.0, A.mult, col(3), A.add)
         ts(v("l4"), v("mi"), 4.0, A.mult, 3.0, A.add)
+        tt(v("mj", 144, 216), v("mj", 72, 144), v("mi"), A.add)
+        tt(v("md", 0, 48), v("mf", 0, 48), v("mf", 24, 72), A.subtract)
+        tt(v("md", 48, 72), v("mf", 0, 24), v("mf", 48, 72), A.subtract)
+        cp(v("lk"), v("mj", 144, 216))
         ts(v("dl"), v("md"), float(C), A.add)
 
     def more_lists():
         ts(v("l3"), v("mi"), 3.0, A.mult, 2.0, A.add)
-        ts(v("m2", 0, 24), v("mf", 48, 72), col(4), A.add, -1.125 * U, A.add)
-        ts(v("m2", 24, 48), v("mf", 48, 72), col(4), A.add)
-        quant("E", 0, 512, v("et"))
+        ts(v("m2", 0, 24), v("mf", 48, 72), col(6), A.add, (3 - SHIFT) * U, A.add)
+        ts(v("m2", 48, 72), v("mf", 48, 72), col(6), A.subtract, 3 * U, A.add)
 
-    def plane(h, b):
-        if b == 0:
-            return v("tt", 3072 * h, 3072 * h + 4 * C, 4)
-        base, t = (0, 12 - b) if b > 8 else ((4 * 384, 8 - b) if b > 4 else (4 * 640, 4 - b))
-        a = 3072 * h + base + t
-        return v("tt", a, a + 4 * 32 * b - t, 4)
+    def plane(b, lo=0, hi=None):
+        s = NBLK - b
+        a = 4 * TILES[s // 4][0] + s % 4
+        return v("tt", a + 4 * lo, a + 4 * (16 * b if hi is None else hi) - s % 4, 4)
 
     def last(name, n=C):
         return v(name, 15, n, 16)
 
-    def sweep(win, lst, into, slots, parts, scale, bias, func, d0, out, o, between=None, after=None, mid=None):
-        def sides(a, b, k):
-            return v(into, slots * a + k, slots * b, slots), [win, v(lst, 24 * k + a // 16, 24 * k + b // 16)]
-        for i, (a, b, vk) in enumerate(parts):
-            for k in range(3):
+    def sweep(win, lst, into, slots, parts, scale, bias, d0, out, o0, o, own=False):
+        for a, b, vk in parts:
+            for k in range(4 if own else 3):
+                if k == 3:
+                    (cp if k in vk else act)(v(d0, slots * a + k, slots * b, slots), [win, v("lo", a // 16, b // 16)])
+                    continue
+                dst, wl = v(into, slots * a + k, slots * b, slots), [win, v(lst, 24 * k + a // 16, 24 * k + b // 16)]
                 if k not in vk:
-                    dst, wl = sides(a, b, k)
-                    act(dst, wl, scale, bias, None, func)
-            if i == 0 and mid is not None:
-                mid()
-        for k in range(3):
-            mine = [p for p in parts if k in p[2]]
-            if mine:
-                dst, wl = sides(mine[0][0], mine[-1][1], k)
-                if bias is None:
-                    cp(dst, wl)
+                    act(dst, wl, scale, bias)
+                elif bias is None:
+                    ts(dst, wl, scale, A.mult)
                 else:
                     ts(dst, wl, scale, A.mult, bias, A.add)
-        if between is not None:
-            between()
-        for a, b, vk in parts:
-            scan(v(out, slots * a, slots * b), v(d0, slots * a, slots * b), v(into, slots * a, slots * b), o)
-            if after is not None:
-                after(a, b)
+            scan(v(out, slots * a, slots * b), v(d0, slots * a, slots * b), v(into, slots * a, slots * b), o, o0)
 
     def a_round(n):
+        mm(0, "UU", 0, "X", 0, H)
         mm(1, "UU", 0, "X", 0, H)
-        mm(0, "UU", 128, "X", 0, H)
-        mm(2, "UU", 128, "X", 0, H)
         mm(4, "UU", 0, "X", 0, C)
-        mm(5, "UU", 128, "X", 0, C)
+        mm(5, "UU", 0, "X", 0, C)
+
+        def own(b):
+            return v("hh", 16 * b + 15, 16 * b + 16)
+
+        def mask(k, a, b):
+            tt(v("ms", a, b), bank(k, b, a), v("mk", a, b), A.min)
+
+        def hold(a, b):
+            scan(v("hh", a, b), v("hd", a, b), v("ms", a, b), A.max)
+
+        def compare(b):
+            ts(plane(b), bank(0 if 16 * b <= H else 4, 16 * b), own(b), A.is_lt, 2.0, A.mult)
+
+        def count(b):
+            scan(v("rj", RW * b + RW - 8 * b, RW * b + RW), plane(b, 0, 8 * b), plane(b, 8 * b), A.add, A.add, 16.0 * (above(b) - b))
+
+        def gap(b):
+            return v("dd", 8 * b * (b - 1), 8 * b * (b + 1))
+
+        def pack(i, j):
+            a, e = TILES[i][0], sum(TILES[j])
+            quant("T", a, e, v("tt", 4 * a, 4 * e))
+            for t in range(i, j + 1):
+                mm(6, "S", 128 * min(t, 1), "T", TILES[t][0], TILES[t][1], t == 0, t == CLOSE[-1][1])
+
+        mask(0, 0, H)
         if n == 0:
             move_lists()
-
-        def own(h, b):
-            return v("dtr", C * h + 32 * b, C * h + 32 * b + 1)
-
-        def pl(h, b):
-            ts(plane(h, b), bank(1 if h == 0 and 32 * b < H else 4 + h, 32 * b), own(h, b), A.is_lt)
-            a = 2112 * h + 16 * b * (b - 1)
-            act(v("junk", a, a + 32 * b), plane(h, b), -STEP, STEP, v("rs", 12 * h + b, 12 * h + b + 1))
-
-        def qa(h):
-            quant("T", 768 * h, 768 * h + C, v("tt", 3072 * h, 3072 * h + 4 * C))
-            mm(6, "S", 128 * h, "T", 768 * h, C, h == 0, h == 1)
-
-        def qbc(h):
-            quant("T", 768 * h + C, 768 * h + 768, v("tt", 3072 * h + 4 * C, 3072 * h + 3072))
-            mm(6, "S", 128 * h, "T", 768 * h + C, 256, False, False)
-            mm(6, "S", 128 * h, "T", 768 * h + 640, 128, False, False)
-
-        def inside(h, a):
-            tt(v("dd", C * h + a, C * h + C), v("dtr", C * h + a, C * h + C), bank(4 + h, C, a), A.subtract)
-
-        def wins(h):
-            tt(plane(h, 0), v("dd", C * h, C * h + C), v("mk"), A.is_gt)
-
-        turn(v("dtr", 0, H), bank(1, H))
-        turn(v("dtr", C, C + H), bank(0, H))
-        for b in range(NB):
-            act(v("dd", C + 32 * b, C + 32 * b + 32), bank(2, 32 * b + 32, 32 * b), -1.0, own(1, b))
-        for b in (7, 6, 5):
-            pl(0, b)
-        turn(v("dtr", H, C), bank(4, C, H))
-        turn(v("dtr", C + H, 2 * C), bank(5, C, H))
-        for b in (4, 3, 2, 1, 11, 10, 9, 8):
-            pl(0, b)
-        inside(0, 0)
-        for b in (11, 10):
-            pl(1, b)
-        wins(0)
-        for b in (9, 8, 7):
-            pl(1, b)
-        qa(0)
-        for b in range(6, 0, -1):
-            pl(1, b)
-        act(v("rx"), [v("rs"), v("xl")], 1.0, YB)
-        inside(1, 32 * NB)
-        qbc(0)
-        wins(1)
-        qbc(1)
-        qa(1)
-        turn(v("rt"), v("rx"))
+        hold(0, H)
+        mask(4, H, C)
+        compare(1)
+        hold(H, C)
+        for i in range(len(THEIRS) + 1):
+            if i < len(THEIRS):
+                b = THEIRS[i]
+                act(gap(b), bank(1 if 16 * b <= H else 5, 16 * b), -1.0, own(b))
+            if i > 0:
+                b = THEIRS[i - 1]
+                act(plane(b), gap(b), 1.0, -TINY, v("rj", RW * b + RW - 1, RW * b + RW), F.Sign)
         if n == 0:
-            act(v("sa", 3, 4 * C, 4), v("bt", 0, C), 1.0, 0.5)
-        tt(v("yy"), bank(6, C), v("rt"), A.add)
+            planes()
+        count(1)
+        tt(plane(NBLK), v("hh"), bank(4, C), A.is_lt)
+        due = []
+        for i, b in enumerate(MINE):
+            if isinstance(b, tuple):
+                pack(*b)
+                continue
+            compare(b)
+            if i == 0:
+                scan(v("sb"), v("sg", 0, 2 * C, 2), plane(NBLK), A.add, A.mult)
+            if i == 2:
+                ts(v("pk", 0, 24), last("sb"), STEP, A.mult, col(8), A.add)
+            if due:
+                count(due.pop())
+            due.append(b)
+        pack(*CLOSE[0])
+        count(due.pop())
+        for x in CLOSE[1:]:
+            pack(*x)
+        ts(v("pk", 24, 48), v("rj", RW - 1, RW * NBLK, RW), -STEP / 2, A.mult)
+        tt(v("pk", 48, 72), v("pk", 0, 24), v("pk", 24, 48), A.add)
+        scan(v("ec"), v("dy"), bank(6, C), A.min)
+        key, lost = v("pk", 72, 96), v("pk", 96, 120)
+        tt(key, last("ec"), v("pk", 48, 72), A.add)
+        ts(lost, key, (C - K - 0.5 - MID) * STEP, A.is_gt, -8 * U, A.mult)
+        ts(v("pl"), key, 1.0 / STEP, A.mult, float(MID), A.add)
+        tt(v("sp", 0, 2 * C, 32), key, lost, A.add)
+        ts(v("sm", 0, 24), key, 1.0 / STEP, A.mult, float(MID + K), A.add)
+        scan(v("sq"), v("sg"), v("sp"), A.add, A.mult)
+        if n == 0:
+            more_lists()
+        row[0] = "keys"
+        turn(v("kw"), v("sq"))
 
-        def labels():
-            act(v("da", 3, 4 * C, 4), v("yy"), -1.0, CUT, None, F.Sign)
-
-        def places():
-            scan(v("ey"), v("dy"), v("yy"), A.min)
-            ts(v("pl"), last("ey"), col(5), A.add, 1.0 / STEP, A.mult)
-            op("V", lambda: g.vector.tensor_copy(ap(v("ow")).indirect(ap(v("pl"))), ap(v("iw", 0, C))),
-               [v("pl"), v("iw", 0, C)], [v("ow")])
-
-        def border():
-            scan(v("eo"), v("de", 0, K), v("ow", 0, K), A.min)
-            ts(v("sm", 0, 24), last("ey"), 1.0 / STEP, A.mult, col(6), A.add)
-            ts(v("ol"), last("eo", K), col(4), A.add)
-            ts(v("sm", 24, 48), last("ey"), col(7), A.add, -8 * U / (STEP / 2), A.mult)
-            for b in range(4):
-                ts(v("bt", b, 4 * K, 4), [v("fp", FW * b, FW * b + C), v("ol")], 1.0 / 32, A.mult)
-            tt(v("sm", 48, 72), v("sm", 0, 24), v("sm", 24, 48), A.max)
-            quant("B", 128 * n, 128 * n + 128, v("bt"))
-            send(n)
-            if n == 0:
-                more_lists()
-
-        def keys(a, b):
-            tt(v("w3", a, b), v("s2", 4 * a + 3, 4 * b, 4), v("yy", a, b), A.min)
-
-        def keys_after(a, b):
-            if a == 0:
-                keys(0, 128)
+        op("V", lambda: g.vector.tensor_copy(ap(v("ow")).indirect(ap(v("pl"))), ap(v("iw", 0, C))),
+           [v("pl"), v("iw", 0, C)], [v("ow")], scatter=1)
+        row[0] = None
+        scan(v("eo"), v("de", 0, K), v("ow", 0, K), A.min)
+        ts(v("ol"), last("eo", K), col(6), A.add)
+        for b in range(4):
+            side = v("bt", b, 4 * K, 4), [v("fp", FW * b, FW * b + C), v("ol")]
+            if b < BV:
+                ts(*side, 1.0 / 32, A.mult)
             else:
-                keys(128, a)
-                keys(a, b)
-
-        def choice():
-            scan(v("e3"), v("de"), v("s3", 2, 3 * C, 3), A.min)
-
-        def reply(a, b):
-            i, j = a // 16, b // 16
-            return [lambda: scan(v("e4", a, b), v("de", a, b), v("s4", 3 * a + 2, 3 * b, 3), A.min),
-                    lambda: tt(v("sm", 120 + i, 120 + j), v("e4", a + 15, b, 16), v("m2", 24 + i, 24 + j), A.add),
-                    lambda: tt(v("ti", i, j), v("sm", 120 + i, 120 + j), v("sm", 96 + i, 96 + j), A.min),
-                    lambda: ts(v("ti", 24 + i, 24 + j), v("ti", i, j), 511, A.bitwise_and),
-                    lambda: cp(v("tl", i, j), v("ti", 24 + i, 24 + j))]
-
-        def held(a, b):
-            if a == 0:
-                tt(v("sm", 72, 96), last("e3"), v("m2", 0, 24), A.add)
-                reply(a, b)[0]()
-                tt(v("sm", 96, 120), v("sm", 72, 96), v("sm", 48, 72), A.min)
-                reply(a, b)[1]()
-            else:
-                first, second = reply(0, a), reply(a, b)
-                for step in (first[2], second[0], first[3], second[1], first[4], second[2], second[3], second[4]):
-                    step()
-
-        sweep(v("yy"), "l1", "sa", 4, PARTS[0], 1.0, -CUT, F.Sign, "da", "s1", A.max, places, None, labels)
+                act(*side, 1.0 / 32)
+        quant("B", 128 * n, 128 * n + 128, v("bt"))
         if n == 0:
-            ts(v("fp", FW * 3, FW * 3 + C), v("xt", 3, 4 * C, 4), 32.0, A.mult)
-        sweep(v("s1"), "l4", "sa", 4, PARTS[1], -1.0, 2.0, F.Sign, "da", "s2", A.max, border, keys_after)
-        if n == 0:
+            late_constants()
+            quant("E", 0, 512, v("et"))
             for k in (1, 2):
                 act(v("dmin", k, 3 * C, 3), [v("iw"), v("dl", 24 * k - 24, 24 * k)], 1.0, -C - PREF)
-        sweep(v("w3"), "l1", "x3", 3, PARTS[2], 2 * U, 2 * U, F.Identity, "dmin", "s3", A.min)
-        if n == 0:
-            for k in (1, 2):
                 act(v("dmax", k, 3 * C, 3), v("dmin", k, 3 * C, 3), 1.0, 2 * PREF)
+            act(v("dmax", 0, 3 * C, 3), v("de"), -1.0)
+            act(v("otb"), [v("iw"), v("dl", 48, 72)], 1.0, 2 * PREF - C)
+            ts(v("yb"), v("de"), -1.0, A.is_gt)
+            scan(v("e4"), v("yb"), v("otb"), A.add, A.mult)
+            ts(v("sm", 48, 72), last("e4"), col(6), A.mult, -1.0 / (LOW * U), A.mult)
+            tt(v("m2", 24, 48), v("m2", 48, 72), v("sm", 48, 72), A.add)
+        send(n)
+        sweep(v("kw"), "lk", "sa", 4, PARTS[0], -1.0 / (8 * U), -1.5, "da", "s1", A.min, A.max, True)
+        sweep(v("s1"), "l4", "sa", 4, PARTS[1], -4.0, -3.0, "da", "s2", A.min, A.max)
+        sweep(v("s2"), "l4", "x3", 3, PARTS[2], U, None, "dmin", "s3", A.add, A.min)
         for b in range(4):
             mm(b, "E", 128 * b, "L", K + K * n, 128)
-        sweep(v("s3"), "l3", "x4", 3, PARTS[3], 1.0, None, F.Identity, "dmax", "s4", A.max, choice, held)
-        for b in range(4):
             act(v("fp", FW * b + C, FW * b + FW), bank(b, 128, 32), 32.0)
-            act(v("gp", FW * b + C, FW * b + FW), bank(b, 128, 32), 0.5)
+            act(v("hp", FW * b + C, FW * b + FW), bank(b, 128, 32), 64.0 if b < 3 else 0.5)
+        sweep(v("s3"), "l3", "x4", 3, PARTS[3], 1.0, None, "dmax", "s4", A.add, A.max)
+        scan(v("e3"), v("de"), v("s3", 2, 3 * C, 3), A.min)
+        tt(v("sm", 24, 48), v("m2", 0, 24), lost, A.add)
+        tt(v("sm", 72, 96), last("e3"), v("sm", 24, 48), A.add)
+        tt(v("sm", 96, 120), v("sm", 72, 96), v("sm", 0, 24), A.max)
+        for a, b in REPLY:
+            i, j = a // 16, b // 16
+            tt(v("sm", 120 + i, 120 + j), v("s4", 3 * a + 47, 3 * b, 48), v("m2", 24 + i, 24 + j), A.add)
+            tt(v("ti", i, j), v("sm", 120 + i, 120 + j), v("sm", 96 + i, 96 + j), A.min)
+            ts(v("ti", 24 + i, 24 + j), v("ti", i, j), 511, A.bitwise_and)
+            cp(v("tl", i, j), v("ti", 24 + i, 24 + j))
 
-        def half(b, lo, hi):
-            return v("gp", FW * b + lo, FW * b + hi), [v("fp", FW * b, FW * b + FW), v("tl", lo // 16, hi // 16)]
+        def picked(name, b, lo, hi):
+            return [v(name, FW * b, FW * b + FW), v("tl", lo // 16, hi // 16)]
 
-        cut = PARTS[3][0][1]
-        for b in range(2):
-            act(*half(b, 0, cut), 1.0 / 64)
-        ts(*half(0, cut, C), 1.0 / 64, A.mult)
-        act(*half(1, cut, C), 1.0 / 64)
-        for b in range(2, 4):
-            act(*half(b, 0, C), 1.0 / 64)
-        act(v("gq", 3 * C, 4 * C), v("gp", 3 * FW, 3 * FW + C))
-
-        def mean(b, lo, hi):
-            tt(v("zt", 4 * lo + b, 4 * hi, 4), [v("gp", FW * b, FW * b + FW), v("tl", lo // 16, hi // 16)],
-               v("gq", C * b + lo, C * b + hi), A.add)
-
-        def twin(b):
-            cp(v("gq", C * b, C * b + C), v("gp", FW * b, FW * b + C))
-
-        twin(0)
-        twin(1)
-        mean(0, 0, C)
-        twin(2)
-        mean(1, 0, C)
-        mean(2, 0, C)
+        row[0] = "layer"
+        for lo, hi in REPLY:
+            act(v("hp", 3 * FW + lo, 3 * FW + hi), picked("fp", 3, lo, hi), 1.0 / 64)
+        for b in range(3):
+            for lo, hi in (REPLY if b < SPLIT else ((0, C),)):
+                tt(v("hp", FW * b + lo, FW * b + hi), picked("fp", b, lo, hi), v("fq", C * b + lo, C * b + hi), A.add)
+            for lo, hi in MEANS[b]:
+                act(v("zt", 4 * lo + b, 4 * hi, 4), picked("hp", b, lo, hi), 1.0 / 64)
+            if b == 1:
+                cp(v("fq", 3 * C, 4 * C), v("hp", 3 * FW, 3 * FW + C))
+        for b, lo, hi in OWN:
+            ts(v("zt", 4 * lo + b, 4 * hi, 4), picked("hp", b, lo, hi), 1.0 / 64, A.mult)
         if n == ROUNDS - 1:
             act(v("otb"), [v("iw"), v("tl")])
             dma("S", lambda: T.ot[:], lambda: ap(v("otb", 0, C, 1, (0, 128, 16))), [v("otb")], [])
 
         for i, (lo, hi) in enumerate(runs):
-            mean(3, lo, hi)
+            tt(v("zt", 4 * lo + 3, 4 * hi, 4), picked("hp", 3, lo, hi), v("fq", 3 * C + lo, 3 * C + hi), A.add)
+        for i, (lo, hi) in enumerate(runs):
             quant("Z", lo, hi, v("zt", 4 * lo, 4 * hi))
             for b in range(4):
                 mm(4 * i + b, "W", 128 * b, "Z", lo, hi - lo)
-        if n == 0:
-            quant("V", 0, 128, v("vt"))
 
         def add(i, b):
             lo, hi = runs[i]
@@ -446,14 +449,21 @@ def rank_program(g, core, T, topo):
 
         for b in range(3):
             act(*add(0, b), 1.0 / 32)
-        late = [add(0, 3), add(1, 0)]
+        late = [add(0, 3), add(1, 0), add(1, 1)]
         ts(*late[0], 1.0 / 32, A.mult)
         act(*late[1], 1.0 / 32)
-        late = [add(1, b) for b in range(1, 4)]
+        late += [add(1, 2), add(1, 3)]
+        ts(*late[2], 1.0 / 32, A.mult)
         quant("X", 0, H, v("xt", 0, 4 * H))
-        for r in late:
+        for r in late[3:]:
             ts(*r, 1.0 / 32, A.mult)
+        row[0] = None
         quant("X", H, C, v("xt", 4 * H, 4 * C))
+        if n == 0:
+            quant("V", 0, 128, v("vt"))
+        if n < ROUNDS - 1:
+            for b in range(3):
+                twin(b)
 
     for n in range(ROUNDS):
         a_round(n)
@@ -468,37 +478,91 @@ def rank_program(g, core, T, topo):
         dma("AS"[i], lambda lo=lo, hi=hi: T.y[:, lo:hi], lambda lo=lo, hi=hi: ap(v("yb", lo, hi)), [v("yb", lo, hi)], [])
 
     names = "VAPGSX"
-    wrote = {b: np.full(s[1][1], -1) for b, s in SCRATCH.items()}
-    read = {b: {q: np.full(s[1][1], -1) for q in names} for b, s in SCRATCH.items()}
-    known = {q: {} for q in names}
-    done, waits, waited = [], [], set()
 
     def cols(r):
         if r[0] == "ps":
             return slice(r[1] // 512 * 512, r[1] // 512 * 512 + 512)
         return slice(r[1], r[2], r[3])
 
+    def needs():
+        wrote = {b: np.full(s[1][1], -1) for b, s in SCRATCH.items()}
+        read = {b: [] for b in SCRATCH}
+        out = []
+        for i, o in enumerate(ops):
+            deps = set()
+            for r in o["r"] + o["w"]:
+                deps.update(int(d) for d in np.unique(wrote[r[0]][cols(r)]))
+            for r in o["w"] + [r for r in o["r"] if r[0] == "ps"]:
+                mark = np.zeros(SCRATCH[r[0]][1][1], bool)
+                mark[cols(r)] = True
+                deps.update(d for d, c in read[r[0]] if mark[c].any() and (r in o["w"] or ops[d]["q"] != o["q"]))
+            for r in o["w"]:
+                wrote[r[0]][cols(r)] = i
+                read[r[0]] = [(d, c) for d, c in read[r[0]] if (wrote[r[0]][c] < d).any()]
+            if o["k"] != "remote":
+                for r in o["r"]:
+                    read[r[0]].append((i, cols(r)))
+            out.append(deps - {-1, i})
+        return out
+
+    def length(o):
+        if o["k"] != "c":
+            return (300, 0) if o["k"] == "remote" else (50, TRIP * (1 + (o["q"] == "X")))
+        n = max(len(range(*r[1:4])) for r in o["w"] + o["r"][-1:] * o["s"])
+        sides = [SCRATCH[r[0]] for r in o["w"] + o["r"] if len(range(*r[1:4])) > 1]
+        if any(SCRATCH[r[0]][2] == U16 for r in o["r"]) and sides[0][2] != U16:
+            return 60 + n * (2.6 if o["s"] else 1.2), 0
+        if o["q"] == "V" and sides and all(s[2] == BF for s in sides):
+            n = n / 2
+        return {"V": max(64, n) * 0.83, "A": 40 + n * 0.83, "P": 0.6 * n + 10, "G": 150 + 1.66 * n}[o["q"]], 60 * (o["q"] == "P")
+
+    deps, true = needs(), needs()
+    for i, o in enumerate(ops):
+        if o["q"] in "GSX" or o["k"] == "dma":
+            deps[i].update([j for j in range(i) if ops[j]["q"] == o["q"] or ops[j]["k"] == "remote"][-1:])
+        if o["row"]:
+            deps[i].update([j for j in range(i) if ops[j]["q"] == o["q"] and ops[j]["row"] == o["row"]][-1:])
+    size = [length(o) for o in ops]
+    after = [set() for o in ops]
+    for i in range(len(ops)):
+        for d in deps[i]:
+            after[d].add(i)
+
+    def lag(d, i):
+        return size[d][1] + WAKE if ops[d]["k"] != "remote" and ops[i]["q"] != ops[d]["q"] or (d in true[i] and ops[i]["q"] != "P") else 0
+
+    def place(order, before, gap):
+        busy, end = {q: [] for q in names}, {}
+        for i in order:
+            t = max([0.0] + [end[d] + gap(d, i) for d in before[i]])
+            line, k = busy[ops[i]["q"]], 0
+            while k < len(line) and line[k][0] < t + size[i][0]:
+                t = max(t, line[k][1])
+                k += 1
+            line.insert(k, (t, t + size[i][0]))
+            end[i] = t + size[i][0]
+        return end
+
+    ahead = [0.0] * len(ops)
+    for i in range(len(ops) - 1, -1, -1):
+        ahead[i] = sum(size[i]) + max([0.0] + [ahead[j] + lag(i, j) - size[i][1] for j in after[i]])
+    end = place(sorted(range(len(ops)), key=lambda i: (-ahead[i], i)), deps, lag)
+    for _ in range(TURNS):
+        back = place(sorted(range(len(ops)), key=lambda i: (-end[i], -i)), after, lambda d, i: lag(i, d))
+        end = place(sorted(range(len(ops)), key=lambda i: (-back[i], i)), deps, lag)
+    ops[:] = [ops[i] for i in sorted(range(len(ops)), key=lambda i: (end[i] - size[i][0], i))]
+
+    deps = needs()
+    known = {q: {} for q in names}
+    done, waits, waited = [], [], set()
+
     def source(d):
         return ops[d]["q"] if ops[d]["k"] == "c" else ops[d]["sem"]
 
     for i, o in enumerate(ops):
-        q, deps, soft = o["q"], set(), set()
-        for r in o["r"]:
-            deps.update(int(d) for d in np.unique(wrote[r[0]][cols(r)]))
-            if r[0] == "ps":
-                for e in names:
-                    if e != q:
-                        deps.add(int(read["ps"][e][cols(r)].max()))
-        for r in o["w"]:
-            soft.update(int(d) for d in np.unique(wrote[r[0]][cols(r)]))
-            for e in names:
-                soft.add(int(read[r[0]][e][cols(r)].max()))
-        for d in soft:
-            if d >= 0 and (ops[d]["q"] != q or q != "P"):
-                deps.add(d)
-        mine = []
-        for d in sorted(deps, reverse=True):
-            if d >= 0 and q != "X" and known[q].get(source(d), -1) < d:
+        q, mine = o["q"], []
+        for d in sorted(deps[i], reverse=True):
+            if q != "X" and not ops[d]["q"] == q == "P" and known[q].get(source(d), -1) < d:
                 mine.append(d)
                 waited.add(d)
                 for s, w in done[d].items():
@@ -507,11 +571,6 @@ def rank_program(g, core, T, topo):
         done.append(dict(known[q]))
         if o["k"] != "remote":
             done[i][source(i)] = i
-        if o["k"] == "c":
-            for r in o["r"]:
-                read[r[0]][q][cols(r)] = i
-        for r in o["w"]:
-            wrote[r[0]][cols(r)] = i
 
     count, total = {}, {q: 0 for q in names}
     for i, o in enumerate(ops):

@@ -3,7 +3,8 @@ from concourse.mybir import dt, AluOpType, ActivationFunctionType
 
 C, K, ROUNDS = 384, 96, 3
 FW = C + K
-H = 256
+CUTS = (0, 128, 256, C)
+SCORES, SUMS = (4, 6, 0), 2
 NBLK = C // 16
 RW = 192
 STEP = 2.0 ** -9
@@ -18,17 +19,18 @@ FILL = 15000000
 TINY = 2.0 ** -120
 X4, U8, BF, F32, I32, U16 = "float8_e4m3fn_x4", "uint8", "bfloat16", "float32", "int32", "uint16"
 TILES = ((0, 384), (384, 320), (704, 256), (960, 192), (1152, 128), (1280, 128))
-THEIRS = (15, 14, 20, 19, 18, 17, 16, 13)
-MINE = (23, 22, 21, 2, (0, 0), 3, 4, 5, 6, 7, 8, 9, 10, 11, (4, 5), 12)
-CLOSE = ((3, 3), (1, 1), (2, 2))
+THEIRS = (7, 6, 5, 15, 14, 20, 19, 18, 17)
+COUNTED = (23, 22)
+PACKS = ((0, 0), (4, 5), (3, 3), (2, 2), (1, 1))
+COPY = ((0, 3), (1, 3), (2, 3))
+NG = 1
 PARTS = (((0, 256, ()), (256, C, (0, 3))), ((0, 224, (0,)), (224, C, (0, 1))),
          ((0, 160, (0,)), (160, 288, (0,)), (288, C, (0,))), ((0, 256, (0,)), (256, C, ())))
 REPLY = ((0, 256), (256, C))
 SPLIT = 1
-MEANS = (((0, C),), ((0, C),), ((0, H), (H, C)))
-OWN = ()
+ZA = ((0, 0, C), (1, 0, 128), (1, 128, C), (2, 0, 128), (2, 128, 256), (2, 256, C))
 BV = 2
-WAKE, TRIP, TURNS = 240, 1500, 2
+WAKE, TRIP, TURNS = 300, 1500, 2
 
 SCRATCH = {"ps": ("psum", [128, 4096], F32)}
 for _n, _w in (("X", C), ("U", 128), ("UU", 128), ("V", 128), ("W", 512), ("E", 512), ("S", 256), ("T", 1408),
@@ -41,8 +43,8 @@ for _n, _w, _d in (("xt", 4 * C, BF), ("ut", 512, BF), ("vt", 512, BF), ("et", 2
                    ("iw", 768, F32), ("pi", 8, I32), ("cl", 16, F32), ("li", 56, I32), ("ul", 8, U16), ("rl", 24, U16),
                    ("lo", 24, U16), ("mi", 72, I32), ("mj", 216, I32), ("mf", 72, F32), ("lk", 72, U16), ("l4", 72, U16),
                    ("l3", 72, U16), ("md", 72, F32), ("dl", 72, U16), ("m2", 72, F32), ("e2", 64, F32), ("pat", 48, F32),
-                   ("mk", C, BF), ("hd", C, BF), ("de", C, BF), ("dy", C, BF), ("sg", 2 * C, BF), ("sp", 2 * C, BF),
-                   ("sq", 2 * C, BF), ("kw", 2 * C, BF), ("ms", C, F32), ("hh", C, F32), ("sb", C, BF),
+                   ("mk", C, BF), ("hd", C, BF), ("de", C, BF), ("dy", C, BF), ("sg", 2 * C + 2, BF), ("sp", 2 * C + 2, BF),
+                   ("sh", C, BF), ("sq", 2 * C + 2, BF), ("kw", 2 * C, BF), ("ms", C, F32), ("hh", C, F32), ("sb", C, BF),
                    ("dd", 16 * 276, BF), ("rj", RW * NBLK, F32), ("ec", C, F32), ("pk", 168, F32),
                    ("da", 4 * C, BF), ("sa", 4 * C, BF), ("s1", 4 * C, BF), ("s2", 4 * C, BF),
                    ("x3", 3 * C, F32), ("s3", 3 * C, F32), ("x4", 3 * C, BF), ("s4", 3 * C, F32),
@@ -51,12 +53,12 @@ for _n, _w, _d in (("xt", 4 * C, BF), ("ut", 512, BF), ("vt", 512, BF), ("et", 2
                    ("ti", 48, I32), ("tl", 24, U16), ("otb", C, F32), ("yb", C, F32)):
     SCRATCH[_n] = ("sbuf", [128, _w], _d)
 
-NDMA = 30
+NDMA = 34
 SEMAPHORES = ["cV", "cA", "cP", "cG", "sent"] + ["arr%d" % n for n in range(ROUNDS)] + ["d%d" % n for n in range(NDMA)]
 
 
 def above(b):
-    return sum(1 for x in range(b + 1, max(THEIRS)) if x not in THEIRS) - max(0, b - max(THEIRS))
+    return sum(1 for x in range(b + 1, NBLK) if x not in THEIRS)
 
 
 def rank_program(g, core, T, topo):
@@ -131,7 +133,7 @@ def rank_program(g, core, T, topo):
         elif bias is not None:
             op("A", lambda: g.scalar.activation(ap(out), src(in_), func, bias=src(bias), scale=scale), regs(in_, bias), [out])
         elif scale != 1.0:
-            op("A", lambda: g.scalar.activation(ap(out), src(in_), F.Copy, scale=scale), regs(in_), [out])
+            op("A", lambda: g.scalar.activation(ap(out), src(in_), F.Copy, scale=src(scale)), regs(in_, scale), [out])
         else:
             op("A", lambda: g.scalar.activation(ap(out), src(in_), F.Copy), regs(in_), [out])
 
@@ -170,7 +172,7 @@ def rank_program(g, core, T, topo):
         op("G", lambda: g.remote_dma(ap(ls), ap(s), sem, T.sem.sent, pid, rid, emask), [s], [], "remote")
         op("X", None, [], [lq, ls], "dma", "arr%d" % n, 2 * len(lanes(origin, core)))
 
-    runs = ((0, H), (H, C))
+    runs = tuple(zip(CUTS, CUTS[1:]))
 
     for a, b in runs:
         dma("S", lambda a=a, b=b: ap(v("xt", 4 * a, 4 * b)), lambda a=a, b=b: T.x[:, 4 * a:4 * b], [], [v("xt", 4 * a, 4 * b)])
@@ -186,9 +188,18 @@ def rank_program(g, core, T, topo):
     iota(v("li", 8, 32), [[0, NBLK]], 0, 1)
     iota(v("li", 32, 56), [[32, NBLK]], 0, 0)
     iota(v("gi"), [[1, 8], [0, 64]], 0, 0)
-    iota(v("sg"), [[0, 2 * C]], 1, 0)
-    iota(v("sg", 0, 2 * C, 32), [[0, NBLK]], 0, 0)
-    iota(v("sp"), [[0, 2 * C]], 0, 0)
+    b = 0
+    while b < NBLK:
+        e = b + 1
+        while e + 1 < NBLK and above(e + 1) - above(e) == above(b + 1) - above(b):
+            e += 1
+        e = min(e, NBLK - 1)
+        iota(v("pk", 144 + b, 145 + e), [[16 * (above(min(b + 1, e)) - above(b)), e + 1 - b]], 16 * above(b), 0)
+        b = e + 1
+    iota(v("sh"), [[0, C]], 1, 0)
+    iota(v("sh", 0, C, 16), [[0, NBLK]], 0, 0)
+    iota(v("sg"), [[0, 2 * C + 2]], 1, 0)
+    iota(v("sp"), [[0, 2 * C + 2]], 0, 0)
     iota(v("iw", 16, 768), [[1, 752]], 16, 0)
     iota(v("da", 0, 4 * C, 4), [[0, C]], -16, 0)
     iota(v("da", 1, 4 * C, 4), [[0, C]], 16, 0)
@@ -218,21 +229,27 @@ def rank_program(g, core, T, topo):
     ts(v("pat", 0, 16), v("e2", 0, 16), 2 * FAR, A.mult, -FAR, A.add)
     ts(v("pat", 16, 32), v("e2", 0, 16), -4 * FAR, A.mult)
     ts(v("e2", 32, 48), v("e2", 0, 16), BIG, A.mult)
-    ts(col(7), col(6), 1.0 / U, A.mult, (8 * max(THEIRS) - MID) * STEP, A.add)
+    ts(col(7), col(6), 1024.0 / U, A.mult, 2.0 * MID - 16 * (NBLK - 1), A.add)
+    for h in range(2):
+        ts(col(9 + h), col(3), 16.0 * h, A.is_equal, -STEP / 2, A.mult)
+        ts(col(11 + h), col(3), 16.0 * h, A.is_equal, -8 * U, A.mult)
+        ts(col(13 + h), col(3), 16.0 * h, A.not_equal)
+        ts(v("sg", 16 * h, 2 * C, 32), v("sg", 16 * h, 2 * C, 32), col(13 + h), A.mult)
     ts(v("pat", 16, 17), v("e2", 0, 1), -6 * FAR, A.mult, 2 * FAR, A.add)
     tt(v("pat", 32, 48), v("e2", 32, 48), v("e2", 16, 32), A.add)
-    ts(col(8), col(2), STEP, A.mult, col(7), A.add)
+    ts(col(8), col(2), -2.0, A.mult, col(7), A.add)
+    ts(v("pk", 120, 144), v("pk", 144, 168), col(8), A.add)
     for k, name in enumerate(("mk", "hd", "de")):
         act(v(name), [v("pat", 16 * k, 16 * k + 16), v("rl")])
     for a, w in TILES[:-1]:
         fill(v("tt", 4 * (a + w - 48), 4 * (a + w)), 0.0)
     fill(v("tt", 4 * TILES[-1][0], 4 * sum(TILES[-1])), 0.0)
-    fill(v("rj", RW - 1, RW), 16.0 * above(0))
+    fill(v("rj", RW - 1, RW), 0.0)
     quant("L", 0, 128, v("bt"))
     ts(v("lo"), v("li", 32, 56), col(1), A.add)
     quant("U", 0, 128, v("ut"))
     for h in range(2):
-        ts(v("st", 512 * h, 512 * h + 512), v("gi"), col(4), A.is_equal, STEP / 2, A.mult)
+        ts(v("st", 512 * h, 512 * h + 512), v("gi"), col(4), A.is_equal, -1.0, A.mult)
     op("V", lambda: g.vector.tensor_copy(ap(v("qUU")).bitcast(dt.uint32), ap(v("qU")).bitcast(dt.uint32).indirect(ap(v("ul")))),
        [v("qU"), v("ul")], [v("qUU")])
     act(v("sUU"), [v("sU"), v("ul")])
@@ -246,10 +263,10 @@ def rank_program(g, core, T, topo):
             [v("fp", FW * b, FW * b + C)], [v("fq", C * b, C * b + C)])
 
     def planes():
-        act(v("dy"), v("de"), 1.0 / U)
+        act(v("dy"), v("de"), 1024.0 / U)
         for b in range(4):
             act(v("fp", FW * b, FW * b + C), v("xt", b, 4 * C, 4), 32.0)
-            if b < 3:
+            if b < 4 - NG:
                 twin(b)
 
     def move_lists():
@@ -292,10 +309,12 @@ def rank_program(g, core, T, topo):
             scan(v(out, slots * a, slots * b), v(d0, slots * a, slots * b), v(into, slots * a, slots * b), o, o0)
 
     def a_round(n):
-        mm(0, "UU", 0, "X", 0, H)
-        mm(1, "UU", 0, "X", 0, H)
-        mm(4, "UU", 0, "X", 0, C)
-        mm(5, "UU", 0, "X", 0, C)
+        for k, (lo, hi) in zip(SCORES, runs):
+            mm(k, "UU", 0, "X", 0, hi)
+            mm(k + 1, "UU", 0, "X", 0, hi)
+
+        def scores(n):
+            return [k for k, (lo, hi) in zip(SCORES, runs) if n <= hi][0]
 
         def own(b):
             return v("hh", 16 * b + 15, 16 * b + 16)
@@ -307,69 +326,72 @@ def rank_program(g, core, T, topo):
             scan(v("hh", a, b), v("hd", a, b), v("ms", a, b), A.max)
 
         def compare(b):
-            ts(plane(b), bank(0 if 16 * b <= H else 4, 16 * b), own(b), A.is_lt, 2.0, A.mult)
-
-        def count(b):
-            scan(v("rj", RW * b + RW - 8 * b, RW * b + RW), plane(b, 0, 8 * b), plane(b, 8 * b), A.add, A.add, 16.0 * (above(b) - b))
+            ts(plane(b), bank(scores(16 * b), 16 * b), own(b), A.is_lt, 2.0, A.mult)
 
         def gap(b):
             return v("dd", 8 * b * (b - 1), 8 * b * (b + 1))
+
+        def total(b):
+            return v("rj", RW * b + RW - 1, RW * b + RW)
+
+        def count(b):
+            if b in COUNTED:
+                act(gap(b), plane(b), 1.0, -1.0, total(b))
+            else:
+                scan(v("rj", RW * b + RW - 8 * b, RW * b + RW), plane(b, 0, 8 * b), plane(b, 8 * b), A.add, A.add, -16.0 * b)
 
         def pack(i, j):
             a, e = TILES[i][0], sum(TILES[j])
             quant("T", a, e, v("tt", 4 * a, 4 * e))
             for t in range(i, j + 1):
-                mm(6, "S", 128 * min(t, 1), "T", TILES[t][0], TILES[t][1], t == 0, t == CLOSE[-1][1])
+                mm(SUMS, "S", 128 * min(t, 1), "T", TILES[t][0], TILES[t][1], t == 0, t == PACKS[-1][1])
 
-        mask(0, 0, H)
-        if n == 0:
-            move_lists()
-        hold(0, H)
-        mask(4, H, C)
-        compare(1)
-        hold(H, C)
+        mine = [b for b in range(NBLK - 1, 0, -1) if b not in THEIRS]
+        early = [b for b in mine if 16 * b < CUTS[-2]]
+        for k, (lo, hi) in zip(SCORES, runs):
+            mask(k, lo, hi)
+            hold(lo, hi)
+        row[0] = "compare"
         for i in range(len(THEIRS) + 1):
             if i < len(THEIRS):
                 b = THEIRS[i]
-                act(gap(b), bank(1 if 16 * b <= H else 5, 16 * b), -1.0, own(b))
+                act(gap(b), bank(scores(16 * b) + 1, 16 * b), -1.0, own(b))
             if i > 0:
                 b = THEIRS[i - 1]
-                act(plane(b), gap(b), 1.0, -TINY, v("rj", RW * b + RW - 1, RW * b + RW), F.Sign)
-        if n == 0:
-            planes()
-        count(1)
-        tt(plane(NBLK), v("hh"), bank(4, C), A.is_lt)
-        due = []
-        for i, b in enumerate(MINE):
-            if isinstance(b, tuple):
-                pack(*b)
-                continue
+                act(plane(b), gap(b), 1.0, -TINY, total(b), F.Sign)
+        for b in early[::-1]:
             compare(b)
-            if i == 0:
-                scan(v("sb"), v("sg", 0, 2 * C, 2), plane(NBLK), A.add, A.mult)
-            if i == 2:
-                ts(v("pk", 0, 24), last("sb"), STEP, A.mult, col(8), A.add)
-            if due:
-                count(due.pop())
-            due.append(b)
-        pack(*CLOSE[0])
-        count(due.pop())
-        for x in CLOSE[1:]:
-            pack(*x)
-        ts(v("pk", 24, 48), v("rj", RW - 1, RW * NBLK, RW), -STEP / 2, A.mult)
-        tt(v("pk", 48, 72), v("pk", 0, 24), v("pk", 24, 48), A.add)
-        scan(v("ec"), v("dy"), bank(6, C), A.min)
-        key, lost = v("pk", 72, 96), v("pk", 96, 120)
-        tt(key, last("ec"), v("pk", 48, 72), A.add)
-        ts(lost, key, (C - K - 0.5 - MID) * STEP, A.is_gt, -8 * U, A.mult)
-        ts(v("pl"), key, 1.0 / STEP, A.mult, float(MID), A.add)
-        tt(v("sp", 0, 2 * C, 32), key, lost, A.add)
-        ts(v("sm", 0, 24), key, 1.0 / STEP, A.mult, float(MID + K), A.add)
-        scan(v("sq"), v("sg"), v("sp"), A.add, A.mult)
+        tt(plane(NBLK), v("hh"), bank(SCORES[-1], C), A.is_lt)
+        steps = [lambda: scan(v("sb"), v("sh"), plane(NBLK), A.add, A.mult),
+                 lambda: ts(v("pk", 0, 24), last("sb"), -2.0, A.mult),
+                 lambda: tt(v("pk", 24, 48), v("pk", 0, 24), v("pk", 120, 144), A.add)]
+        for b in mine[:len(mine) - len(early)]:
+            compare(b)
+            if steps:
+                steps.pop(0)()
+        row[0] = None
         if n == 0:
+            move_lists()
+            planes()
             more_lists()
+        for b in mine:
+            count(b)
+        for x in PACKS:
+            pack(*x)
+        scan(v("ec"), v("dy"), bank(SUMS, C), A.min)
+        twice, lost = v("pk", 72, 96), v("pk", 96, 120)
+        cut = 2.0 * (MID + K - C) + 1
+        tt(v("pk", 48, 72), v("pk", 24, 48), v("rj", RW - 1, RW * NBLK, RW), A.add)
+        tt(twice, v("pk", 48, 72), last("ec"), A.add)
+        for h in range(2):
+            act(v("sp", 16 * h, 2 * C, 32), twice, col(9 + h))
+            ts(v("sp", 16 * h + 1, 2 * C, 32), twice, cut, A.is_lt, col(11 + h), A.mult)
+        ts(v("pl"), twice, -0.5, A.mult, float(MID), A.add)
+        ts(lost, twice, cut, A.is_lt, -8 * U, A.mult)
+        act(v("sm", 0, 24), twice, -0.5, float(MID + K))
+        scan(v("sq"), v("sg"), v("sp"), A.add, A.mult)
         row[0] = "keys"
-        turn(v("kw"), v("sq"))
+        turn(v("kw"), v("sq", 2, 2 * C + 2))
 
         op("V", lambda: g.vector.tensor_copy(ap(v("ow")).indirect(ap(v("pl"))), ap(v("iw", 0, C))),
            [v("pl"), v("iw", 0, C)], [v("ow")], scatter=1)
@@ -402,7 +424,7 @@ def rank_program(g, core, T, topo):
         for b in range(4):
             mm(b, "E", 128 * b, "L", K + K * n, 128)
             act(v("fp", FW * b + C, FW * b + FW), bank(b, 128, 32), 32.0)
-            act(v("hp", FW * b + C, FW * b + FW), bank(b, 128, 32), 64.0 if b < 3 else 0.5)
+            act(v("hp", FW * b + C, FW * b + FW), bank(b, 128, 32), 64.0 if b < 4 - NG else 0.5)
         sweep(v("s3"), "l3", "x4", 3, PARTS[3], 1.0, None, "dmax", "s4", A.add, A.max)
         scan(v("e3"), v("de"), v("s3", 2, 3 * C, 3), A.min)
         tt(v("sm", 24, 48), v("m2", 0, 24), lost, A.add)
@@ -419,50 +441,43 @@ def rank_program(g, core, T, topo):
             return [v(name, FW * b, FW * b + FW), v("tl", lo // 16, hi // 16)]
 
         row[0] = "layer"
-        for lo, hi in REPLY:
-            act(v("hp", 3 * FW + lo, 3 * FW + hi), picked("fp", 3, lo, hi), 1.0 / 64)
-        for b in range(3):
+        for b in range(4 - NG, 4):
+            for lo, hi in (REPLY if b == 4 - NG else ((0, C),)):
+                act(v("hp", b * FW + lo, b * FW + hi), picked("fp", b, lo, hi), 1.0 / 64)
+        for b in range(4 - NG):
             for lo, hi in (REPLY if b < SPLIT else ((0, C),)):
                 tt(v("hp", FW * b + lo, FW * b + hi), picked("fp", b, lo, hi), v("fq", C * b + lo, C * b + hi), A.add)
-            for lo, hi in MEANS[b]:
-                act(v("zt", 4 * lo + b, 4 * hi, 4), picked("hp", b, lo, hi), 1.0 / 64)
             if b == 1:
-                cp(v("fq", 3 * C, 4 * C), v("hp", 3 * FW, 3 * FW + C))
-        for b, lo, hi in OWN:
-            ts(v("zt", 4 * lo + b, 4 * hi, 4), picked("hp", b, lo, hi), 1.0 / 64, A.mult)
+                for k in range(4 - NG, 4):
+                    cp(v("fq", k * C, k * C + C), v("hp", k * FW, k * FW + C))
+        for b, lo, hi in ZA:
+            act(v("zt", 4 * lo + b, 4 * hi, 4), picked("hp", b, lo, hi), 1.0 / 64)
+        for lo, hi in runs:
+            for b in range(4 - NG, 4):
+                tt(v("zt", 4 * lo + b, 4 * hi, 4), picked("hp", b, lo, hi), v("fq", b * C + lo, b * C + hi), A.add)
+        row[0] = None
         if n == ROUNDS - 1:
             act(v("otb"), [v("iw"), v("tl")])
             dma("S", lambda: T.ot[:], lambda: ap(v("otb", 0, C, 1, (0, 128, 16))), [v("otb")], [])
 
         for i, (lo, hi) in enumerate(runs):
-            tt(v("zt", 4 * lo + 3, 4 * hi, 4), picked("hp", 3, lo, hi), v("fq", 3 * C + lo, 3 * C + hi), A.add)
-        for i, (lo, hi) in enumerate(runs):
             quant("Z", lo, hi, v("zt", 4 * lo, 4 * hi))
             for b in range(4):
-                mm(4 * i + b, "W", 128 * b, "Z", lo, hi - lo)
-
-        def add(i, b):
-            lo, hi = runs[i]
-            f = v("fp", FW * b + lo, FW * b + hi)
-            tt(f, bank(4 * i + b, hi - lo), f, A.add)
-            return v("xt", 4 * lo + b, 4 * hi, 4), f
-
-        for b in range(3):
-            act(*add(0, b), 1.0 / 32)
-        late = [add(0, 3), add(1, 0), add(1, 1)]
-        ts(*late[0], 1.0 / 32, A.mult)
-        act(*late[1], 1.0 / 32)
-        late += [add(1, 2), add(1, 3)]
-        ts(*late[2], 1.0 / 32, A.mult)
-        quant("X", 0, H, v("xt", 0, 4 * H))
-        for r in late[3:]:
-            ts(*r, 1.0 / 32, A.mult)
-        row[0] = None
-        quant("X", H, C, v("xt", 4 * H, 4 * C))
+                mm(4 * (i % 2) + b, "W", 128 * b, "Z", lo, hi - lo)
+            for b in range(4):
+                f, x = v("fp", FW * b + lo, FW * b + hi), v("xt", 4 * lo + b, 4 * hi, 4)
+                row[0] = "adds"
+                tt(f, bank(4 * (i % 2) + b, hi - lo), f, A.add)
+                row[0] = None
+                if (i, b) in COPY:
+                    ts(x, f, 1.0 / 32, A.mult)
+                else:
+                    act(x, f, 1.0 / 32)
+            quant("X", lo, hi, v("xt", 4 * lo, 4 * hi))
         if n == 0:
             quant("V", 0, 128, v("vt"))
         if n < ROUNDS - 1:
-            for b in range(3):
+            for b in range(4 - NG):
                 twin(b)
 
     for n in range(ROUNDS):
@@ -470,12 +485,12 @@ def rank_program(g, core, T, topo):
 
     for i, (lo, hi) in enumerate(runs):
         mm(i, "V", 0, "X", lo, hi - lo)
-        dma("SA"[i], lambda lo=lo, hi=hi: T.oc[:, 4 * lo:4 * hi], lambda lo=lo, hi=hi: codes(v("qX", lo, hi)), [v("qX", lo, hi)], [])
+        dma("SA"[i % 2], lambda lo=lo, hi=hi: T.oc[:, 4 * lo:4 * hi], lambda lo=lo, hi=hi: codes(v("qX", lo, hi)), [v("qX", lo, hi)], [])
     for k in range(4):
         dma("SA"[k // 2], lambda k=k: T.osc[4 * k:4 * k + 4, :], lambda k=k: ap(v("sX", 0, C, 1, (32 * k, 32 * k + 4))), [v("sX")], [])
     for i, (lo, hi) in enumerate(runs):
         cp(v("yb", lo, hi), bank(i, hi - lo))
-        dma("AS"[i], lambda lo=lo, hi=hi: T.y[:, lo:hi], lambda lo=lo, hi=hi: ap(v("yb", lo, hi)), [v("yb", lo, hi)], [])
+        dma("AS"[i % 2], lambda lo=lo, hi=hi: T.y[:, lo:hi], lambda lo=lo, hi=hi: ap(v("yb", lo, hi)), [v("yb", lo, hi)], [])
 
     names = "VAPGSX"
 
@@ -507,7 +522,8 @@ def rank_program(g, core, T, topo):
 
     def length(o):
         if o["k"] != "c":
-            return (300, 0) if o["k"] == "remote" else (50, TRIP * (1 + (o["q"] == "X")))
+            wide = sum(len(range(*r[1:4])) for r in o["w"])
+            return (300, 0) if o["k"] == "remote" else (50, 2 * TRIP if o["q"] == "X" else TRIP + wide)
         n = max(len(range(*r[1:4])) for r in o["w"] + o["r"][-1:] * o["s"])
         sides = [SCRATCH[r[0]] for r in o["w"] + o["r"] if len(range(*r[1:4])) > 1]
         if any(SCRATCH[r[0]][2] == U16 for r in o["r"]) and sides[0][2] != U16:

@@ -19,38 +19,39 @@ FILL = 15000000
 TINY = 2.0 ** -120
 X4, U8, BF, F32, I32, U16 = "float8_e4m3fn_x4", "uint8", "bfloat16", "float32", "int32", "uint16"
 TILES = ((0, 384), (384, 320), (704, 256), (960, 192), (1152, 128), (1280, 128))
-THEIRS = (7, 6, 5, 15, 14, 20, 19, 18, 17)
-COUNTED = (23, 22)
+THEIRS = (7, 6, 15, 14, 20, 19, 18, 17)
+COUNTED = (1, 2, 3, 4, 5, 8, 9)
 PACKS = ((0, 0), (4, 5), (3, 3), (2, 2), (1, 1))
 COPY = ((0, 3), (1, 3), (2, 3))
 NG = 1
-PARTS = (((0, 256, ()), (256, C, (0, 3))), ((0, 224, (0,)), (224, C, (0, 1))),
-         ((0, 160, (0,)), (160, 288, (0,)), (288, C, (0,))), ((0, 256, (0,)), (256, C, ())))
-REPLY = ((0, 256), (256, C))
-SPLIT = 1
-ZA = ((0, 0, C), (1, 0, 128), (1, 128, C), (2, 0, 128), (2, 128, 256), (2, 256, C))
-BV = 2
-WAKE, TRIP, TURNS = 300, 1500, 2
+PARTS = (((0, 256, ()), (256, C, (0, 3))), ((0, 192, (0,)), (192, C, (0, 1))),
+         ((0, 160, (0, 1)), (160, 288, (0,)), (288, C, ())), ((0, 128, (0,)), (128, 288, (0,)), (288, C, ())))
+REPLY = ((0, 128), (128, C))
+SPLIT = 2
+ZA = ((0, 0, C), (1, 0, 256), (2, 0, 128), (2, 128, 256), (1, 256, C), (2, 256, C))
+BV = 1
+FLIGHT = (3500, 2600)
+WAKE, TRIP, TURNS = 260, 1300, 2
 
 SCRATCH = {"ps": ("psum", [128, 4096], F32)}
 for _n, _w in (("X", C), ("U", 128), ("UU", 128), ("V", 128), ("W", 512), ("E", 512), ("S", 256), ("T", 1408),
                ("B", 128 * ROUNDS), ("L", 128 + K * ROUNDS), ("Z", C)):
     SCRATCH["q" + _n] = ("sbuf", [128, _w], X4)
     SCRATCH["s" + _n] = ("sbuf", [128, _w], U8)
-for _n, _w, _d in (("xt", 4 * C, BF), ("ut", 512, BF), ("vt", 512, BF), ("et", 2048, BF), ("st", 1024, BF), ("gi", 512, BF),
+for _n, _w, _d in (("xt", 4 * C, BF), ("ut", 512, BF), ("vt", 512, BF), ("et", 1040, BF), ("st", 1024, BF), ("gi", 512, BF),
                    ("tt", 4 * 1408, BF), ("bt", 512, BF), ("zt", 4 * C, BF), ("fp", 4 * FW, BF), ("fq", 4 * C, BF),
                    ("hp", 4 * FW, BF),
                    ("iw", 768, F32), ("pi", 8, I32), ("cl", 16, F32), ("li", 56, I32), ("ul", 8, U16), ("rl", 24, U16),
                    ("lo", 24, U16), ("mi", 72, I32), ("mj", 216, I32), ("mf", 72, F32), ("lk", 72, U16), ("l4", 72, U16),
-                   ("l3", 72, U16), ("md", 72, F32), ("dl", 72, U16), ("m2", 72, F32), ("e2", 64, F32), ("pat", 48, F32),
-                   ("mk", C, BF), ("hd", C, BF), ("de", C, BF), ("dy", C, BF), ("sg", 2 * C + 2, BF), ("sp", 2 * C + 2, BF),
+                   ("l3", 72, U16), ("md", 72, F32), ("dl", 72, U16), ("m2", 72, F32), ("e2", 64, F32), ("pat", 64, F32),
+                   ("mk", C, BF), ("hd", C, BF), ("de", C, BF), ("sg", 2 * C + 2, BF), ("sp", 2 * C + 2, BF),
                    ("sh", C, BF), ("sq", 2 * C + 2, BF), ("kw", 2 * C, BF), ("ms", C, F32), ("hh", C, F32), ("sb", C, BF),
-                   ("dd", 16 * 276, BF), ("rj", RW * NBLK, F32), ("ec", C, F32), ("pk", 168, F32),
+                   ("dd", 16 * 276, BF), ("rj", NBLK, F32), ("rb", RW * NBLK, BF), ("ec", C, F32), ("pk", 168, F32),
                    ("da", 4 * C, BF), ("sa", 4 * C, BF), ("s1", 4 * C, BF), ("s2", 4 * C, BF),
                    ("x3", 3 * C, F32), ("s3", 3 * C, F32), ("x4", 3 * C, BF), ("s4", 3 * C, F32),
                    ("dmin", 3 * C, F32), ("dmax", 3 * C, F32), ("eo", K, F32), ("e3", C, F32),
                    ("e4", C, F32), ("pl", 24, U16), ("ow", C, F32), ("ol", 6, U16), ("sm", 144, F32),
-                   ("ti", 48, I32), ("tl", 24, U16), ("otb", C, F32), ("yb", C, F32)):
+                   ("ti", 72, I32), ("rp", 48, F32), ("tl", 24, U16), ("otb", C, F32), ("yb", C, F32)):
     SCRATCH[_n] = ("sbuf", [128, _w], _d)
 
 NDMA = 34
@@ -171,13 +172,14 @@ def rank_program(g, core, T, topo):
         op("G", lambda: g.remote_dma(codes(lq), codes(q), sem, T.sem.sent, pid, rid, emask), [q], [], "remote")
         op("G", lambda: g.remote_dma(ap(ls), ap(s), sem, T.sem.sent, pid, rid, emask), [s], [], "remote")
         op("X", None, [], [lq, ls], "dma", "arr%d" % n, 2 * len(lanes(origin, core)))
+        ops[-1]["far"] = FLIGHT[min(n, 1)]
 
     runs = tuple(zip(CUTS, CUTS[1:]))
 
-    for a, b in runs:
+    dma("S", lambda: ap(v("ut")), lambda: T.u[:], [], [v("ut")])
+    for a, b in ((0, CUTS[1]), (CUTS[1], C)):
         dma("S", lambda a=a, b=b: ap(v("xt", 4 * a, 4 * b)), lambda a=a, b=b: T.x[:, 4 * a:4 * b], [], [v("xt", 4 * a, 4 * b)])
-    dma("A", lambda: ap(v("ut")), lambda: T.u[:], [], [v("ut")])
-    dma("A", lambda: ap(v("mi")), lambda: T.mv[:], [], [v("mi")])
+    dma("S", lambda: ap(v("mi")), lambda: T.mv[:], [], [v("mi")])
     dma("S", lambda: codes(v("qW")), lambda: T.wc[:], [v("xt")], [v("qW")])
     dma("S", lambda: ap(v("sW")), lambda: T.ws[:], [], [v("sW")])
     dma("S", lambda: ap(v("vt")), lambda: T.v[:], [], [v("vt")])
@@ -187,37 +189,36 @@ def rank_program(g, core, T, topo):
     iota(v("li", 0, 8), [[16, 8]], 0, 0)
     iota(v("li", 8, 32), [[0, NBLK]], 0, 1)
     iota(v("li", 32, 56), [[32, NBLK]], 0, 0)
-    iota(v("gi"), [[1, 8], [0, 64]], 0, 0)
+    iota(v("tt", 4 * TILES[-1][0], 4 * sum(TILES[-1])), [[0, 512]], 0, 0)
     b = 0
     while b < NBLK:
         e = b + 1
         while e + 1 < NBLK and above(e + 1) - above(e) == above(b + 1) - above(b):
             e += 1
         e = min(e, NBLK - 1)
-        iota(v("pk", 144 + b, 145 + e), [[16 * (above(min(b + 1, e)) - above(b)), e + 1 - b]], 16 * above(b), 0)
+        iota(v("pk", 144 + b, 145 + e), [[16 * (above(min(b + 1, e)) - above(b)), e + 1 - b]], 16 * (above(b) - NBLK + 1) + 2 * MID, 0)
         b = e + 1
     iota(v("sh"), [[0, C]], 1, 0)
+    iota(v("gi"), [[1, 8], [0, 64]], 0, 0)
     iota(v("sh", 0, C, 16), [[0, NBLK]], 0, 0)
-    iota(v("sg"), [[0, 2 * C + 2]], 1, 0)
     iota(v("sp"), [[0, 2 * C + 2]], 0, 0)
+    for h in range(2):
+        e, z = v("et", 520 * h, 520 * h + 514), v("sp", 0, 514)
+        op("G", lambda e=e, z=z, h=h: g.affine_select(ap(e), ap(z), [[-1, 514]], A.not_equal, 1.0, 2 + h, 4), [z], [e])
+    iota(v("sg"), [[0, 2 * C + 2]], 1, 0)
     iota(v("iw", 16, 768), [[1, 752]], 16, 0)
-    iota(v("da", 0, 4 * C, 4), [[0, C]], -16, 0)
-    iota(v("da", 1, 4 * C, 4), [[0, C]], 16, 0)
-    iota(v("da", 2, 4 * C, 4), [[0, C]], 16, 0)
     iota(v("sa", 3, 4 * C, 4), [[0, C]], -2, 0)
-
-    def late_constants():
-        for b in range(4):
-            e = v("et", 513 * b, 512 * b + 512, 4)
-            op("G", lambda e=e: g.affine_select(ap(e), ap(e), [[1, 128]], A.not_equal, 1.0, 0, -1), [e], [e])
-        iota(v("dmin", 0, 3 * C, 3), [[0, C]], FILL, 0)
-
-    fill(v("et"), 0.0)
+    iota(v("dmin", 0, 3 * C, 3), [[0, C]], FILL, 0)
+    row[0] = "first"
+    fill(v("bt"), 0.0)
     ts(v("pi", 1, 2), v("pi", 0, 1), 31, A.bitwise_and)
+    row[0] = None
+    for name, k, c in (("da", 0, -16.0), ("da", 1, 16.0), ("da", 2, 16.0)):
+        act(v(name, k, 4 * C, 4), v("bt", 0, C), 1.0, c)
+
     ts(v("pi", 2, 3), v("pi", 0, 1), 15, A.bitwise_and)
     ts(v("pi", 3, 4), v("pi", 0, 1), 16, A.bitwise_and)
     ts(v("pi", 4, 5), v("pi", 0, 1), 4, A.arith_shift_right)
-    fill(v("bt"), 0.0)
     cp(v("cl", 0, 5), v("pi", 0, 5))
     cp(v("ul"), v("li", 0, 8))
     ts(v("li", 8, 32), v("li", 8, 32), 15, A.bitwise_and)
@@ -229,7 +230,6 @@ def rank_program(g, core, T, topo):
     ts(v("pat", 0, 16), v("e2", 0, 16), 2 * FAR, A.mult, -FAR, A.add)
     ts(v("pat", 16, 32), v("e2", 0, 16), -4 * FAR, A.mult)
     ts(v("e2", 32, 48), v("e2", 0, 16), BIG, A.mult)
-    ts(col(7), col(6), 1024.0 / U, A.mult, 2.0 * MID - 16 * (NBLK - 1), A.add)
     for h in range(2):
         ts(col(9 + h), col(3), 16.0 * h, A.is_equal, -STEP / 2, A.mult)
         ts(col(11 + h), col(3), 16.0 * h, A.is_equal, -8 * U, A.mult)
@@ -237,14 +237,15 @@ def rank_program(g, core, T, topo):
         ts(v("sg", 16 * h, 2 * C, 32), v("sg", 16 * h, 2 * C, 32), col(13 + h), A.mult)
     ts(v("pat", 16, 17), v("e2", 0, 1), -6 * FAR, A.mult, 2 * FAR, A.add)
     tt(v("pat", 32, 48), v("e2", 32, 48), v("e2", 16, 32), A.add)
-    ts(col(8), col(2), -2.0, A.mult, col(7), A.add)
+    ts(v("pat", 48, 64), v("iw", 0, 16), col(5), A.not_equal)
+    ts(col(8), col(2), -2.0, A.mult, col(6), A.add)
     ts(v("pk", 120, 144), v("pk", 144, 168), col(8), A.add)
     for k, name in enumerate(("mk", "hd", "de")):
         act(v(name), [v("pat", 16 * k, 16 * k + 16), v("rl")])
     for a, w in TILES[:-1]:
         fill(v("tt", 4 * (a + w - 48), 4 * (a + w)), 0.0)
-    fill(v("tt", 4 * TILES[-1][0], 4 * sum(TILES[-1])), 0.0)
-    fill(v("rj", RW - 1, RW), 0.0)
+    fill(v("rj"), 0.0)
+    fill(v("rb", RW - 1, RW * NBLK, RW), 0.0)
     quant("L", 0, 128, v("bt"))
     ts(v("lo"), v("li", 32, 56), col(1), A.add)
     quant("U", 0, 128, v("ut"))
@@ -263,7 +264,6 @@ def rank_program(g, core, T, topo):
             [v("fp", FW * b, FW * b + C)], [v("fq", C * b, C * b + C)])
 
     def planes():
-        act(v("dy"), v("de"), 1024.0 / U)
         for b in range(4):
             act(v("fp", FW * b, FW * b + C), v("xt", b, 4 * C, 4), 32.0)
             if b < 4 - NG:
@@ -283,7 +283,7 @@ def rank_program(g, core, T, topo):
     def more_lists():
         ts(v("l3"), v("mi"), 3.0, A.mult, 2.0, A.add)
         ts(v("m2", 0, 24), v("mf", 48, 72), col(6), A.add, (3 - SHIFT) * U, A.add)
-        ts(v("m2", 48, 72), v("mf", 48, 72), col(6), A.subtract, 3 * U, A.add)
+        ts(v("m2", 48, 72), v("mf", 48, 72), col(6), A.subtract)
 
     def plane(b, lo=0, hi=None):
         s = NBLK - b
@@ -294,21 +294,29 @@ def rank_program(g, core, T, topo):
         return v(name, 15, n, 16)
 
     def sweep(win, lst, into, slots, parts, scale, bias, d0, out, o0, o, own=False):
+        todo = [(a, b, k, False) for a, b, vk in parts for k in range(4 if own else 3) if k not in vk]
+        for k in range(4):
+            mine = [p for p in parts if k in p[2]]
+            if len(mine) > 2:
+                todo.append((0, C, k, True))
+            else:
+                todo += [(p[0], p[1], k, True) for p in mine]
+        for a, b, k, vector in todo:
+            if k == 3:
+                (cp if vector else act)(v(d0, slots * a + k, slots * b, slots), [win, v("lo", a // 16, b // 16)])
+                continue
+            dst, wl = v(into, slots * a + k, slots * b, slots), [win, v(lst, 24 * k + a // 16, 24 * k + b // 16)]
+            if not vector:
+                act(dst, wl, scale, bias)
+            elif bias is None:
+                ts(dst, wl, scale, A.mult)
+            else:
+                ts(dst, wl, scale, A.mult, bias, A.add)
         for a, b, vk in parts:
-            for k in range(4 if own else 3):
-                if k == 3:
-                    (cp if k in vk else act)(v(d0, slots * a + k, slots * b, slots), [win, v("lo", a // 16, b // 16)])
-                    continue
-                dst, wl = v(into, slots * a + k, slots * b, slots), [win, v(lst, 24 * k + a // 16, 24 * k + b // 16)]
-                if k not in vk:
-                    act(dst, wl, scale, bias)
-                elif bias is None:
-                    ts(dst, wl, scale, A.mult)
-                else:
-                    ts(dst, wl, scale, A.mult, bias, A.add)
             scan(v(out, slots * a, slots * b), v(d0, slots * a, slots * b), v(into, slots * a, slots * b), o, o0)
 
     def a_round(n):
+        mm(3, "UU", 0, "X", CUTS[-2], C - CUTS[-2])
         for k, (lo, hi) in zip(SCORES, runs):
             mm(k, "UU", 0, "X", 0, hi)
             mm(k + 1, "UU", 0, "X", 0, hi)
@@ -320,7 +328,7 @@ def rank_program(g, core, T, topo):
             return v("hh", 16 * b + 15, 16 * b + 16)
 
         def mask(k, a, b):
-            tt(v("ms", a, b), bank(k, b, a), v("mk", a, b), A.min)
+            tt(v("ms", a, b), bank(k, b, a) if b < C else bank(3, b - a), v("mk", a, b), A.min)
 
         def hold(a, b):
             scan(v("hh", a, b), v("hd", a, b), v("ms", a, b), A.max)
@@ -332,13 +340,15 @@ def rank_program(g, core, T, topo):
             return v("dd", 8 * b * (b - 1), 8 * b * (b + 1))
 
         def total(b):
-            return v("rj", RW * b + RW - 1, RW * b + RW)
+            return v("rj", b, b + 1)
 
         def count(b):
             if b in COUNTED:
+                row[0] = "compare"
                 act(gap(b), plane(b), 1.0, -1.0, total(b))
+                row[0] = None
             else:
-                scan(v("rj", RW * b + RW - 8 * b, RW * b + RW), plane(b, 0, 8 * b), plane(b, 8 * b), A.add, A.add, -16.0 * b)
+                scan(v("rb", RW * b + RW - 8 * b, RW * b + RW), plane(b, 0, 8 * b), plane(b, 8 * b), A.add, A.add, -16.0 * b)
 
         def pack(i, j):
             a, e = TILES[i][0], sum(TILES[j])
@@ -374,20 +384,24 @@ def rank_program(g, core, T, topo):
             move_lists()
             planes()
             more_lists()
-        for b in mine:
+        for b in mine[::-1]:
             count(b)
         for x in PACKS:
             pack(*x)
-        scan(v("ec"), v("dy"), bank(SUMS, C), A.min)
+        scan(v("ec"), v("de"), bank(SUMS, C), A.min)
         twice, lost = v("pk", 72, 96), v("pk", 96, 120)
         cut = 2.0 * (MID + K - C) + 1
-        tt(v("pk", 48, 72), v("pk", 24, 48), v("rj", RW - 1, RW * NBLK, RW), A.add)
+        tt(v("pk", 0, 24), v("pk", 24, 48), v("rj"), A.add)
+        tt(v("pk", 48, 72), v("pk", 0, 24), v("rb", RW - 1, RW * NBLK, RW), A.add)
         tt(twice, v("pk", 48, 72), last("ec"), A.add)
         for h in range(2):
-            act(v("sp", 16 * h, 2 * C, 32), twice, col(9 + h))
+            if h == 0:
+                ts(v("sp", 0, 2 * C, 32), twice, col(9), A.mult)
+            else:
+                act(v("sp", 16, 2 * C, 32), twice, col(10))
             ts(v("sp", 16 * h + 1, 2 * C, 32), twice, cut, A.is_lt, col(11 + h), A.mult)
         ts(v("pl"), twice, -0.5, A.mult, float(MID), A.add)
-        ts(lost, twice, cut, A.is_lt, -8 * U, A.mult)
+        act(lost, twice, -8 * U, 8 * U * cut, None, F.Relu)
         act(v("sm", 0, 24), twice, -0.5, float(MID + K))
         scan(v("sq"), v("sg"), v("sp"), A.add, A.mult)
         row[0] = "keys"
@@ -406,17 +420,19 @@ def rank_program(g, core, T, topo):
                 act(*side, 1.0 / 32)
         quant("B", 128 * n, 128 * n + 128, v("bt"))
         if n == 0:
-            late_constants()
-            quant("E", 0, 512, v("et"))
+            for b in range(4):
+                a = 520 * (b % 2) + 2 * (b < 2)
+                quant("E", 128 * b, 128 * b + 128, v("et", a, a + 512))
             for k in (1, 2):
                 act(v("dmin", k, 3 * C, 3), [v("iw"), v("dl", 24 * k - 24, 24 * k)], 1.0, -C - PREF)
                 act(v("dmax", k, 3 * C, 3), v("dmin", k, 3 * C, 3), 1.0, 2 * PREF)
             act(v("dmax", 0, 3 * C, 3), v("de"), -1.0)
             act(v("otb"), [v("iw"), v("dl", 48, 72)], 1.0, 2 * PREF - C)
-            ts(v("yb"), v("de"), -1.0, A.is_gt)
-            scan(v("e4"), v("yb"), v("otb"), A.add, A.mult)
+            act(v("yb"), [v("pat", 48, 64), v("rl")])
+            for a in (0, C // 2):
+                scan(v("e4", a, a + C // 2), v("yb", a, a + C // 2), v("otb", a, a + C // 2), A.add, A.mult)
             ts(v("sm", 48, 72), last("e4"), col(6), A.mult, -1.0 / (LOW * U), A.mult)
-            tt(v("m2", 24, 48), v("m2", 48, 72), v("sm", 48, 72), A.add)
+            tt(v("rp", 0, 48, 2), v("m2", 48, 72), v("sm", 48, 72), A.add)
         send(n)
         sweep(v("kw"), "lk", "sa", 4, PARTS[0], -1.0 / (8 * U), -1.5, "da", "s1", A.min, A.max, True)
         sweep(v("s1"), "l4", "sa", 4, PARTS[1], -4.0, -3.0, "da", "s2", A.min, A.max)
@@ -425,17 +441,16 @@ def rank_program(g, core, T, topo):
             mm(b, "E", 128 * b, "L", K + K * n, 128)
             act(v("fp", FW * b + C, FW * b + FW), bank(b, 128, 32), 32.0)
             act(v("hp", FW * b + C, FW * b + FW), bank(b, 128, 32), 64.0 if b < 4 - NG else 0.5)
-        sweep(v("s3"), "l3", "x4", 3, PARTS[3], 1.0, None, "dmax", "s4", A.add, A.max)
+        sweep(v("s3"), "l3", "x4", 3, PARTS[3], 1.0, 3 * U, "dmax", "s4", A.add, A.max)
         scan(v("e3"), v("de"), v("s3", 2, 3 * C, 3), A.min)
-        tt(v("sm", 24, 48), v("m2", 0, 24), lost, A.add)
+        tt(v("sm", 24, 48), v("m2", 0, 24), lost, A.subtract)
         tt(v("sm", 72, 96), last("e3"), v("sm", 24, 48), A.add)
-        tt(v("sm", 96, 120), v("sm", 72, 96), v("sm", 0, 24), A.max)
+        tt(v("rp", 1, 48, 2), v("sm", 72, 96), v("sm", 0, 24), A.max)
         for a, b in REPLY:
             i, j = a // 16, b // 16
-            tt(v("sm", 120 + i, 120 + j), v("s4", 3 * a + 47, 3 * b, 48), v("m2", 24 + i, 24 + j), A.add)
-            tt(v("ti", i, j), v("sm", 120 + i, 120 + j), v("sm", 96 + i, 96 + j), A.min)
-            ts(v("ti", 24 + i, 24 + j), v("ti", i, j), 511, A.bitwise_and)
-            cp(v("tl", i, j), v("ti", 24 + i, 24 + j))
+            scan(v("ti", 2 * i, 2 * j), v("s4", 3 * a + 23, 3 * b, 24), v("rp", 2 * i, 2 * j), A.min)
+            ts(v("ti", 48 + i, 48 + j), v("ti", 2 * i + 1, 2 * j, 2), 511, A.bitwise_and)
+            cp(v("tl", i, j), v("ti", 48 + i, 48 + j))
 
         def picked(name, b, lo, hi):
             return [v(name, FW * b, FW * b + FW), v("tl", lo // 16, hi // 16)]
@@ -444,12 +459,17 @@ def rank_program(g, core, T, topo):
         for b in range(4 - NG, 4):
             for lo, hi in (REPLY if b == 4 - NG else ((0, C),)):
                 act(v("hp", b * FW + lo, b * FW + hi), picked("fp", b, lo, hi), 1.0 / 64)
+        for b in range(SPLIT):
+            lo, hi = REPLY[0]
+            tt(v("hp", FW * b + lo, FW * b + hi), picked("fp", b, lo, hi), v("fq", C * b + lo, C * b + hi), A.add)
         for b in range(4 - NG):
-            for lo, hi in (REPLY if b < SPLIT else ((0, C),)):
+            for lo, hi in (REPLY[1:] if b < SPLIT else ((0, C),)):
                 tt(v("hp", FW * b + lo, FW * b + hi), picked("fp", b, lo, hi), v("fq", C * b + lo, C * b + hi), A.add)
             if b == 1:
                 for k in range(4 - NG, 4):
-                    cp(v("fq", k * C, k * C + C), v("hp", k * FW, k * FW + C))
+                    for lo, hi in REPLY:
+                        o, i = v("fq", k * C + lo, k * C + hi), v("hp", k * FW + lo, k * FW + hi)
+                        op("G", lambda o=o, i=i, w=hi - lo: g.affine_select(ap(o), ap(i), [[0, w]], A.is_equal, 0.0, 0, 0), [i], [o])
         for b, lo, hi in ZA:
             act(v("zt", 4 * lo + b, 4 * hi, 4), picked("hp", b, lo, hi), 1.0 / 64)
         for lo, hi in runs:
@@ -484,13 +504,21 @@ def rank_program(g, core, T, topo):
         a_round(n)
 
     for i, (lo, hi) in enumerate(runs):
-        mm(i, "V", 0, "X", lo, hi - lo)
-        dma("SA"[i % 2], lambda lo=lo, hi=hi: T.oc[:, 4 * lo:4 * hi], lambda lo=lo, hi=hi: codes(v("qX", lo, hi)), [v("qX", lo, hi)], [])
-    for k in range(4):
-        dma("SA"[k // 2], lambda k=k: T.osc[4 * k:4 * k + 4, :], lambda k=k: ap(v("sX", 0, C, 1, (32 * k, 32 * k + 4))), [v("sX")], [])
-    for i, (lo, hi) in enumerate(runs):
-        cp(v("yb", lo, hi), bank(i, hi - lo))
-        dma("AS"[i % 2], lambda lo=lo, hi=hi: T.y[:, lo:hi], lambda lo=lo, hi=hi: ap(v("yb", lo, hi)), [v("yb", lo, hi)], [])
+        mm(4 + i, "V", 0, "X", lo, hi - lo)
+        (cp if hi == C else act)(v("yb", lo, hi), bank(4 + i, hi - lo))
+
+    def store(q, name, lo, hi):
+        if name == "oc":
+            dma(q, lambda: T.oc[:, 4 * lo:4 * hi], lambda: codes(v("qX", lo, hi)), [v("qX", lo, hi)], [])
+        elif name == "y":
+            dma(q, lambda: T.y[:, lo:hi], lambda: ap(v("yb", lo, hi)), [v("yb", lo, hi)], [])
+        else:
+            dma(q, lambda: T.osc[4 * lo:4 * hi, :], lambda: ap(v("sX", 0, C, 1, (32 * lo, 32 * lo + 4))), [v("sX")], [])
+        ops[-1]["far"] = TRIP + 4 * (hi - lo)
+
+    for side in (("S", "oc", 0, CUTS[-2]), ("A", "y", 0, CUTS[-2]), ("S", "oc", CUTS[-2], C), ("S", "osc", 0, 1), ("A", "osc", 1, 2),
+                 ("S", "osc", 2, 3), ("A", "osc", 3, 4), ("S", "y", CUTS[-2], C)):
+        store(*side)
 
     names = "VAPGSX"
 
@@ -523,14 +551,14 @@ def rank_program(g, core, T, topo):
     def length(o):
         if o["k"] != "c":
             wide = sum(len(range(*r[1:4])) for r in o["w"])
-            return (300, 0) if o["k"] == "remote" else (50, 2 * TRIP if o["q"] == "X" else TRIP + wide)
+            return (300, 0) if o["k"] == "remote" else (50, o.get("far", TRIP + wide))
         n = max(len(range(*r[1:4])) for r in o["w"] + o["r"][-1:] * o["s"])
         sides = [SCRATCH[r[0]] for r in o["w"] + o["r"] if len(range(*r[1:4])) > 1]
         if any(SCRATCH[r[0]][2] == U16 for r in o["r"]) and sides[0][2] != U16:
-            return 60 + n * (2.6 if o["s"] else 1.2), 0
+            return 60 + n * (2.8 if o["s"] else 1.25), 0
         if o["q"] == "V" and sides and all(s[2] == BF for s in sides):
             n = n / 2
-        return {"V": max(64, n) * 0.83, "A": 40 + n * 0.83, "P": 0.6 * n + 10, "G": 150 + 1.66 * n}[o["q"]], 60 * (o["q"] == "P")
+        return {"V": max(64, n) * 0.83, "A": 50 + max(64, n) * 0.83, "P": 0.6 * n + 10, "G": 150 + 1.66 * n}[o["q"]], 150 * (o["q"] == "P")
 
     deps, true = needs(), needs()
     for i, o in enumerate(ops):
@@ -550,7 +578,7 @@ def rank_program(g, core, T, topo):
     def place(order, before, gap):
         busy, end = {q: [] for q in names}, {}
         for i in order:
-            t = max([0.0] + [end[d] + gap(d, i) for d in before[i]])
+            t = max([size[i][1] if before is after else 0.0] + [end[d] + gap(d, i) for d in before[i]])
             line, k = busy[ops[i]["q"]], 0
             while k < len(line) and line[k][0] < t + size[i][0]:
                 t = max(t, line[k][1])

import numpy as np
from concourse.mybir import dt, AluOpType, ActivationFunctionType

C, K, ROUNDS = 384, 96, 3
FW = C + K
CUTS = (0, 128, 256, C)
SCORES, SUMS = (4, 6, 0), 2
NBLK = C // 16
RW = 192
STEP = 2.0 ** -9
MID = 192
U = float(2 ** 21)
LOW = 3.0
SHIFT = 19.0 / 32
PREF = 512.0
BIG = float(2 ** 26)
FAR = 2.0 ** 90
FILL = 15000000
TINY = 2.0 ** -120
X4, U8, BF, F32, I32, U16 = "float8_e4m3fn_x4", "uint8", "bfloat16", "float32", "int32", "uint16"
TILES = ((0, 384), (384, 320), (704, 256), (960, 192), (1152, 128), (1280, 128))
THEIRS = (7, 6, 15, 14, 20, 19, 18, 17)
COUNTED = (1, 2, 3, 4, 5, 8, 9)
PACKS = ((0, 0), (4, 5), (3, 3), (2, 2), (1, 1))
COPY = ((0, 3), (1, 3), (2, 3))
NG = 1
PARTS = (((0, 256, ()), (256, C, (0, 3))), ((0, 192, (0,)), (192, C, (0, 1))),
         ((0, 160, (0, 1)), (160, 288, (0,)), (288, C, ())), ((0, 128, (0,)), (128, 288, (0,)), (288, C, ())))
REPLY = ((0, 128), (128, C))
SPLIT = 2
ZA = ((0, 0, C), (1, 0, 256), (2, 0, 128), (2, 128, 256), (1, 256, C), (2, 256, C))
BV = 1
FLIGHT = (3500, 2600)
WAKE, TRIP, TURNS = 260, 1300, 2

SCRATCH = {"ps": ("psum", [128, 4096], F32)}
for _n, _w in (("X", C), ("U", 128), ("UU", 128), ("V", 128), ("W", 512), ("E", 512), ("S", 256), ("T", 1408),
               ("B", 128 * ROUNDS), ("L", 128 + K * ROUNDS), ("Z", C)):
    SCRATCH["q" + _n] = ("sbuf", [128, _w], X4)
    SCRATCH["s" + _n] = ("sbuf", [128, _w], U8)
for _n, _w, _d in (("xt", 4 * C, BF), ("ut", 512, BF), ("vt", 512, BF), ("et", 1040, BF), ("st", 1024, BF), ("gi", 512, BF),
                   ("tt", 4 * 1408, BF), ("bt", 512, BF), ("zt", 4 * C, BF), ("fp", 4 * FW, BF), ("fq", 4 * C, BF),
                   ("hp", 4 * FW, BF),
                   ("iw", 768, F32), ("pi", 8, I32), ("cl", 16, F32), ("li", 56, I32), ("ul", 8, U16), ("rl", 24, U16),
                   ("lo", 24, U16), ("mi", 72, I32), ("mj", 216, I32), ("mf", 72, F32), ("lk", 72, U16), ("l4", 72, U16),
                   ("l3", 72, U16), ("md", 72, F32), ("dl", 72, U16), ("m2", 72, F32), ("e2", 64, F32), ("pat", 64, F32),
                   ("mk", C, BF), ("hd", C, BF), ("de", C, BF), ("sg", 2 * C + 2, BF), ("sp", 2 * C + 2, BF),
                   ("sh", C, BF), ("sq", 2 * C + 2, BF), ("kw", 2 * C, BF), ("ms", C, F32), ("hh", C, F32), ("sb", C, BF),
                   ("dd", 16 * 276, BF), ("rj", NBLK, F32), ("rb", RW * NBLK, BF), ("ec", C, F32), ("pk", 168, F32),
                   ("da", 4 * C, BF), ("sa", 4 * C, BF), ("s1", 4 * C, BF), ("s2", 4 * C, BF),
                   ("x3", 3 * C, F32), ("s3", 3 * C, F32), ("x4", 3 * C, BF), ("s4", 3 * C, F32),
                   ("dmin", 3 * C, F32), ("dmax", 3 * C, F32), ("eo", K, F32), ("e3", C, F32),
                   ("e4", C, F32), ("pl", 24, U16), ("ow", C, F32), ("ol", 6, U16), ("sm", 144, F32),
                   ("ti", 72, I32), ("rp", 48, F32), ("tl", 24, U16), ("otb", C, F32), ("yb", C, F32)):
    SCRATCH[_n] = ("sbuf", [128, _w], _d)

NDMA = 34
SEMAPHORES = ["cV", "cA", "cP", "cG", "sent"] + ["arr%d" % n for n in range(ROUNDS)] + ["d%d" % n for n in range(NDMA)]


def above(b):
    return sum(1 for x in range(b + 1, NBLK) if x not in THEIRS)


def rank_program(g, core, T, topo):
    rank = T.rank_of(core)
    if rank is None:
        return
    A, F = AluOpType, ActivationFunctionType
    queue = {"V": g.vector, "A": g.scalar, "P": g.tensor, "G": g, "S": g.sync}
    ops = []

    def v(name, a=0, b=None, s=1, p=None):
        return (name, a, SCRATCH[name][1][1] if b is None else b, s, p)

    def ap(r):
        rows = slice(0, 128) if r[4] is None else slice(*r[4])
        return T[r[0]][rows, r[1]:r[2]:r[3]] if r[3] != 1 else T[r[0]][rows, r[1]:r[2]]

    def bank(k, n, a=0):
        return v("ps", 512 * k + a, 512 * k + n)

    def col(k):
        return v("cl", k, k + 1)

    def src(r):
        if isinstance(r, list):
            return ap(r[0]).indirect(ap(r[1]))
        return ap(r) if isinstance(r, tuple) else r

    def regs(*rs):
        out = []
        for r in rs:
            if isinstance(r, list):
                out += r
            elif isinstance(r, tuple):
                out.append(r)
        return out

    def op(q, f, reads, writes, kind="c", sem=None, count=0, scatter=0):
        ops.append({"q": q, "f": f, "r": reads, "w": writes, "k": kind, "sem": sem, "n": count, "s": scatter, "row": row[0]})

    row = [None]

    def ts(out, in0, s1, op0, s2=None, op1=None):
        if op1 is None:
            op("V", lambda: g.vector.tensor_scalar(ap(out), src(in0), src(s1), None, op0), regs(in0, s1), [out])
        else:
            op("V", lambda: g.vector.tensor_scalar(ap(out), src(in0), src(s1), src(s2), op0, op1), regs(in0, s1, s2), [out])

    def tt(out, in0, in1, o):
        op("V", lambda: g.vector.tensor_tensor(ap(out), src(in0), ap(in1), o), regs(in0, in1), [out])

    def cp(out, in_):
        op("V", lambda: g.vector.tensor_copy(ap(out), src(in_)), regs(in_), [out])

    def fill(out, c):
        op("V", lambda: g.vector.memset(ap(out), c), [], [out])

    def scan(out, d0, d1, o, o0=A.add, first=0.0):
        op("V", lambda: g.vector.tensor_tensor_scan(ap(out), ap(d0), ap(d1), first, o0, o), [d0, d1], [out])

    def turn(out, in_):
        op("V", lambda: g.vector.transpose(ap(out), ap(in_)), [in_], [out])

    def quant(n, a, b, in_):
        q, s = v("q" + n, a, b), v("s" + n, a, b)
        op("V", lambda: g.vector.quantize_mx(ap(q), ap(s), ap(in_)), [in_], [q, s])

    def act(out, in_, scale=1.0, bias=None, accum=None, func=F.Identity):
        if accum is not None:
            op("A", lambda: g.scalar.activation(ap(out), src(in_), func, bias=bias, scale=scale, accum_out=ap(accum)),
               regs(in_), [out, accum])
        elif bias is not None:
            op("A", lambda: g.scalar.activation(ap(out), src(in_), func, bias=src(bias), scale=scale), regs(in_, bias), [out])
        elif scale != 1.0:
            op("A", lambda: g.scalar.activation(ap(out), src(in_), F.Copy, scale=src(scale)), regs(in_, scale), [out])
        else:
            op("A", lambda: g.scalar.activation(ap(out), src(in_), F.Copy), regs(in_), [out])

    def mm(k, w, wa, m, ma, n, start=True, stop=True):
        r = [v("q" + w, wa, wa + 128), v("s" + w, wa, wa + 128), v("q" + m, ma, ma + n), v("s" + m, ma, ma + n)]
        op("P", lambda: g.tensor.matmul_mx(ap(bank(k, n)), ap(r[0]), ap(r[1]), ap(r[2]), ap(r[3]), start, stop), r, [bank(k, n)])

    def iota(out, pattern, base, cm):
        if SCRATCH[out[0]][2] == I32:
            op("G", lambda: g.iota(ap(out), pattern, base, cm), [], [out])
        else:
            op("G", lambda: g.iota(ap(out), pattern, base, cm, allow_small_or_imprecise_dtypes=True), [], [out])

    ndma = [0]

    def dma(q, out, in_, reads, writes):
        op(q, lambda: queue[q].dma_start(out(), in_()), reads, writes, "dma", "d%d" % ndma[0], 16)
        ndma[0] += 1

    def codes(r):
        return ap(r).bitcast(dt.uint8)

    def lanes(a, b):
        return topo.engines(a, b)[:8]

    dest = T.cores[(rank - 1) % len(T.cores)]
    origin = T.cores[(rank + 1) % len(T.cores)]
    rid, pid, _ = topo.addr(dest)
    emask = sum(1 << e for e in lanes(core, dest))

    def send(n):
        q, s = v("qB", 128 * n, 128 * n + K), v("sB", 128 * n, 128 * n + K)
        lq, ls = v("qL", 128 + K * n, 128 + K * n + K), v("sL", 128 + K * n, 128 + K * n + K)
        sem = T.sem["arr%d" % n]
        op("G", lambda: g.remote_dma(codes(lq), codes(q), sem, T.sem.sent, pid, rid, emask), [q], [], "remote")
        op("G", lambda: g.remote_dma(ap(ls), ap(s), sem, T.sem.sent, pid, rid, emask), [s], [], "remote")
        op("X", None, [], [lq, ls], "dma", "arr%d" % n, 2 * len(lanes(origin, core)))
        ops[-1]["far"] = FLIGHT[min(n, 1)]

    runs = tuple(zip(CUTS, CUTS[1:]))

    dma("S", lambda: ap(v("ut")), lambda: T.u[:], [], [v("ut")])
    for a, b in ((0, CUTS[1]), (CUTS[1], C)):
        dma("S", lambda a=a, b=b: ap(v("xt", 4 * a, 4 * b)), lambda a=a, b=b: T.x[:, 4 * a:4 * b], [], [v("xt", 4 * a, 4 * b)])
    dma("S", lambda: ap(v("mi")), lambda: T.mv[:], [], [v("mi")])
    dma("S", lambda: codes(v("qW")), lambda: T.wc[:], [v("xt")], [v("qW")])
    dma("S", lambda: ap(v("sW")), lambda: T.ws[:], [], [v("sW")])
    dma("S", lambda: ap(v("vt")), lambda: T.v[:], [], [v("vt")])

    iota(v("pi", 0, 1), [[0, 1]], 0, 1)
    iota(v("iw", 0, 16), [[1, 16]], 0, 0)
    iota(v("li", 0, 8), [[16, 8]], 0, 0)
    iota(v("li", 8, 32), [[0, NBLK]], 0, 1)
    iota(v("li", 32, 56), [[32, NBLK]], 0, 0)
    iota(v("tt", 4 * TILES[-1][0], 4 * sum(TILES[-1])), [[0, 512]], 0, 0)
    b = 0
    while b < NBLK:
        e = b + 1
        while e + 1 < NBLK and above(e + 1) - above(e) == above(b + 1) - above(b):
            e += 1
        e = min(e, NBLK - 1)
        iota(v("pk", 144 + b, 145 + e), [[16 * (above(min(b + 1, e)) - above(b)), e + 1 - b]], 16 * (above(b) - NBLK + 1) + 2 * MID, 0)
        b = e + 1
    iota(v("sh"), [[0, C]], 1, 0)
    iota(v("gi"), [[1, 8], [0, 64]], 0, 0)
    iota(v("sh", 0, C, 16), [[0, NBLK]], 0, 0)
    iota(v("sp"), [[0, 2 * C + 2]], 0, 0)
    for h in range(2):
        e, z = v("et", 520 * h, 520 * h + 514), v("sp", 0, 514)
        op("G", lambda e=e, z=z, h=h: g.affine_select(ap(e), ap(z), [[-1, 514]], A.not_equal, 1.0, 2 + h, 4), [z], [e])
    iota(v("sg"), [[0, 2 * C + 2]], 1, 0)
    iota(v("iw", 16, 768), [[1, 752]], 16, 0)
    iota(v("sa", 3, 4 * C, 4), [[0, C]], -2, 0)
    iota(v("dmin", 0, 3 * C, 3), [[0, C]], FILL, 0)
    row[0] = "first"
    fill(v("bt"), 0.0)
    ts(v("pi", 1, 2), v("pi", 0, 1), 31, A.bitwise_and)
    row[0] = None
    for name, k, c in (("da", 0, -16.0), ("da", 1, 16.0), ("da", 2, 16.0)):
        act(v(name, k, 4 * C, 4), v("bt", 0, C), 1.0, c)

    ts(v("pi", 2, 3), v("pi", 0, 1), 15, A.bitwise_and)
    ts(v("pi", 3, 4), v("pi", 0, 1), 16, A.bitwise_and)
    ts(v("pi", 4, 5), v("pi", 0, 1), 4, A.arith_shift_right)
    cp(v("cl", 0, 5), v("pi", 0, 5))
    cp(v("ul"), v("li", 0, 8))
    ts(v("li", 8, 32), v("li", 8, 32), 15, A.bitwise_and)
    ts(col(5), col(2), 1.0, A.add)
    ts(v("e2", 0, 16), v("iw", 0, 16), col(2), A.is_equal)
    ts(col(6), col(2), 14.5, A.is_lt, LOW * U, A.mult)
    cp(v("rl"), v("li", 8, 32))
    ts(v("e2", 16, 32), v("iw", 0, 16), col(5), A.is_equal, -LOW * U, A.mult)
    ts(v("pat", 0, 16), v("e2", 0, 16), 2 * FAR, A.mult, -FAR, A.add)
    ts(v("pat", 16, 32), v("e2", 0, 16), -4 * FAR, A.mult)
    ts(v("e2", 32, 48), v("e2", 0, 16), BIG, A.mult)
    for h in range(2):
        ts(col(9 + h), col(3), 16.0 * h, A.is_equal, -STEP / 2, A.mult)
        ts(col(11 + h), col(3), 16.0 * h, A.is_equal, -8 * U, A.mult)
        ts(col(13 + h), col(3), 16.0 * h, A.not_equal)
        ts(v("sg", 16 * h, 2 * C, 32), v("sg", 16 * h, 2 * C, 32), col(13 + h), A.mult)
    ts(v("pat", 16, 17), v("e2", 0, 1), -6 * FAR, A.mult, 2 * FAR, A.add)
    tt(v("pat", 32, 48), v("e2", 32, 48), v("e2", 16, 32), A.add)
    ts(v("pat", 48, 64), v("iw", 0, 16), col(5), A.not_equal)
    ts(col(8), col(2), -2.0, A.mult, col(6), A.add)
    ts(v("pk", 120, 144), v("pk", 144, 168), col(8), A.add)
    for k, name in enumerate(("mk", "hd", "de")):
        act(v(name), [v("pat", 16 * k, 16 * k + 16), v("rl")])
    for a, w in TILES[:-1]:
        fill(v("tt", 4 * (a + w - 48), 4 * (a + w)), 0.0)
    fill(v("rj"), 0.0)
    fill(v("rb", RW - 1, RW * NBLK, RW), 0.0)
    quant("L", 0, 128, v("bt"))
    ts(v("lo"), v("li", 32, 56), col(1), A.add)
    quant("U", 0, 128, v("ut"))
    for h in range(2):
        ts(v("st", 512 * h, 512 * h + 512), v("gi"), col(4), A.is_equal, -1.0, A.mult)
    op("V", lambda: g.vector.tensor_copy(ap(v("qUU")).bitcast(dt.uint32), ap(v("qU")).bitcast(dt.uint32).indirect(ap(v("ul")))),
       [v("qU"), v("ul")], [v("qUU")])
    act(v("sUU"), [v("sU"), v("ul")])
    ts(v("st", 0, 512, 4), v("st", 0, 512, 4), -2.0, A.mult)
    for a, b in runs:
        quant("X", a, b, v("xt", 4 * a, 4 * b))
    quant("S", 0, 256, v("st"))

    def twin(b):
        dma("S", lambda: ap(v("fq", C * b, C * b + C)), lambda: ap(v("fp", FW * b, FW * b + C)),
            [v("fp", FW * b, FW * b + C)], [v("fq", C * b, C * b + C)])

    def planes():
        for b in range(4):
            act(v("fp", FW * b, FW * b + C), v("xt", b, 4 * C, 4), 32.0)
            if b < 4 - NG:
                twin(b)

    def move_lists():
        ts(v("mj", 0, 72), v("mi"), 4, A.arith_shift_right)
        cp(v("mf"), v("mi"))
        ts(v("mj", 72, 144), v("mj", 0, 72), 16.0, A.mult, col(3), A.add)
        ts(v("l4"), v("mi"), 4.0, A.mult, 3.0, A.add)
        tt(v("mj", 144, 216), v("mj", 72, 144), v("mi"), A.add)
        tt(v("md", 0, 48), v("mf", 0, 48), v("mf", 24, 72), A.subtract)
        tt(v("md", 48, 72), v("mf", 0, 24), v("mf", 48, 72), A.subtract)
        cp(v("lk"), v("mj", 144, 216))
        ts(v("dl"), v("md"), float(C), A.add)

    def more_lists():
        ts(v("l3"), v("mi"), 3.0, A.mult, 2.0, A.add)
        ts(v("m2", 0, 24), v("mf", 48, 72), col(6), A.add, (3 - SHIFT) * U, A.add)
        ts(v("m2", 48, 72), v("mf", 48, 72), col(6), A.subtract)

    def plane(b, lo=0, hi=None):
        s = NBLK - b
        a = 4 * TILES[s // 4][0] + s % 4
        return v("tt", a + 4 * lo, a + 4 * (16 * b if hi is None else hi) - s % 4, 4)

    def last(name, n=C):
        return v(name, 15, n, 16)

    def sweep(win, lst, into, slots, parts, scale, bias, d0, out, o0, o, own=False):
        todo = [(a, b, k, False) for a, b, vk in parts for k in range(4 if own else 3) if k not in vk]
        for k in range(4):
            mine = [p for p in parts if k in p[2]]
            if len(mine) > 2:
                todo.append((0, C, k, True))
            else:
                todo += [(p[0], p[1], k, True) for p in mine]
        for a, b, k, vector in todo:
            if k == 3:
                (cp if vector else act)(v(d0, slots * a + k, slots * b, slots), [win, v("lo", a // 16, b // 16)])
                continue
            dst, wl = v(into, slots * a + k, slots * b, slots), [win, v(lst, 24 * k + a // 16, 24 * k + b // 16)]
            if not vector:
                act(dst, wl, scale, bias)
            elif bias is None:
                ts(dst, wl, scale, A.mult)
            else:
                ts(dst, wl, scale, A.mult, bias, A.add)
        for a, b, vk in parts:
            scan(v(out, slots * a, slots * b), v(d0, slots * a, slots * b), v(into, slots * a, slots * b), o, o0)

    def a_round(n):
        mm(3, "UU", 0, "X", CUTS[-2], C - CUTS[-2])
        for k, (lo, hi) in zip(SCORES, runs):
            mm(k, "UU", 0, "X", 0, hi)
            mm(k + 1, "UU", 0, "X", 0, hi)

        def scores(n):
            return [k for k, (lo, hi) in zip(SCORES, runs) if n <= hi][0]

        def own(b):
            return v("hh", 16 * b + 15, 16 * b + 16)

        def mask(k, a, b):
            tt(v("ms", a, b), bank(k, b, a) if b < C else bank(3, b - a), v("mk", a, b), A.min)

        def hold(a, b):
            scan(v("hh", a, b), v("hd", a, b), v("ms", a, b), A.max)

        def compare(b):
            ts(plane(b), bank(scores(16 * b), 16 * b), own(b), A.is_lt, 2.0, A.mult)

        def gap(b):
            return v("dd", 8 * b * (b - 1), 8 * b * (b + 1))

        def total(b):
            return v("rj", b, b + 1)

        def count(b):
            if b in COUNTED:
                row[0] = "compare"
                act(gap(b), plane(b), 1.0, -1.0, total(b))
                row[0] = None
            else:
                scan(v("rb", RW * b + RW - 8 * b, RW * b + RW), plane(b, 0, 8 * b), plane(b, 8 * b), A.add, A.add, -16.0 * b)

        def pack(i, j):
            a, e = TILES[i][0], sum(TILES[j])
            quant("T", a, e, v("tt", 4 * a, 4 * e))
            for t in range(i, j + 1):
                mm(SUMS, "S", 128 * min(t, 1), "T", TILES[t][0], TILES[t][1], t == 0, t == PACKS[-1][1])

        mine = [b for b in range(NBLK - 1, 0, -1) if b not in THEIRS]
        early = [b for b in mine if 16 * b < CUTS[-2]]
        for k, (lo, hi) in zip(SCORES, runs):
            mask(k, lo, hi)
            hold(lo, hi)
        row[0] = "compare"
        for i in range(len(THEIRS) + 1):
            if i < len(THEIRS):
                b = THEIRS[i]
                act(gap(b), bank(scores(16 * b) + 1, 16 * b), -1.0, own(b))
            if i > 0:
                b = THEIRS[i - 1]
                act(plane(b), gap(b), 1.0, -TINY, total(b), F.Sign)
        for b in early[::-1]:
            compare(b)
        tt(plane(NBLK), v("hh"), bank(SCORES[-1], C), A.is_lt)
        steps = [lambda: scan(v("sb"), v("sh"), plane(NBLK), A.add, A.mult),
                 lambda: ts(v("pk", 0, 24), last("sb"), -2.0, A.mult),
                 lambda: tt(v("pk", 24, 48), v("pk", 0, 24), v("pk", 120, 144), A.add)]
        for b in mine[:len(mine) - len(early)]:
            compare(b)
            if steps:
                steps.pop(0)()
        row[0] = None
        if n == 0:
            move_lists()
            planes()
            more_lists()
        for b in mine[::-1]:
            count(b)
        for x in PACKS:
            pack(*x)
        scan(v("ec"), v("de"), bank(SUMS, C), A.min)
        twice, lost = v("pk", 72, 96), v("pk", 96, 120)
        cut = 2.0 * (MID + K - C) + 1
        tt(v("pk", 0, 24), v("pk", 24, 48), v("rj"), A.add)
        tt(v("pk", 48, 72), v("pk", 0, 24), v("rb", RW - 1, RW * NBLK, RW), A.add)
        tt(twice, v("pk", 48, 72), last("ec"), A.add)
        for h in range(2):
            if h == 0:
                ts(v("sp", 0, 2 * C, 32), twice, col(9), A.mult)
            else:
                act(v("sp", 16, 2 * C, 32), twice, col(10))
            ts(v("sp", 16 * h + 1, 2 * C, 32), twice, cut, A.is_lt, col(11 + h), A.mult)
        ts(v("pl"), twice, -0.5, A.mult, float(MID), A.add)
        act(lost, twice, -8 * U, 8 * U * cut, None, F.Relu)
        act(v("sm", 0, 24), twice, -0.5, float(MID + K))
        scan(v("sq"), v("sg"), v("sp"), A.add, A.mult)
        row[0] = "keys"
        turn(v("kw"), v("sq", 2, 2 * C + 2))

        op("V", lambda: g.vector.tensor_copy(ap(v("ow")).indirect(ap(v("pl"))), ap(v("iw", 0, C))),
           [v("pl"), v("iw", 0, C)], [v("ow")], scatter=1)
        row[0] = None
        scan(v("eo"), v("de", 0, K), v("ow", 0, K), A.min)
        ts(v("ol"), last("eo", K), col(6), A.add)
        for b in range(4):
            side = v("bt", b, 4 * K, 4), [v("fp", FW * b, FW * b + C), v("ol")]
            if b < BV:
                ts(*side, 1.0 / 32, A.mult)
            else:
                act(*side, 1.0 / 32)
        quant("B", 128 * n, 128 * n + 128, v("bt"))
        if n == 0:
            for b in range(4):
                a = 520 * (b % 2) + 2 * (b < 2)
                quant("E", 128 * b, 128 * b + 128, v("et", a, a + 512))
            for k in (1, 2):
                act(v("dmin", k, 3 * C, 3), [v("iw"), v("dl", 24 * k - 24, 24 * k)], 1.0, -C - PREF)
                act(v("dmax", k, 3 * C, 3), v("dmin", k, 3 * C, 3), 1.0, 2 * PREF)
            act(v("dmax", 0, 3 * C, 3), v("de"), -1.0)
            act(v("otb"), [v("iw"), v("dl", 48, 72)], 1.0, 2 * PREF - C)
            act(v("yb"), [v("pat", 48, 64), v("rl")])
            for a in (0, C // 2):
                scan(v("e4", a, a + C // 2), v("yb", a, a + C // 2), v("otb", a, a + C // 2), A.add, A.mult)
            ts(v("sm", 48, 72), last("e4"), col(6), A.mult, -1.0 / (LOW * U), A.mult)
            tt(v("rp", 0, 48, 2), v("m2", 48, 72), v("sm", 48, 72), A.add)
        send(n)
        sweep(v("kw"), "lk", "sa", 4, PARTS[0], -1.0 / (8 * U), -1.5, "da", "s1", A.min, A.max, True)
        sweep(v("s1"), "l4", "sa", 4, PARTS[1], -4.0, -3.0, "da", "s2", A.min, A.max)
        sweep(v("s2"), "l4", "x3", 3, PARTS[2], U, None, "dmin", "s3", A.add, A.min)
        for b in range(4):
            mm(b, "E", 128 * b, "L", K + K * n, 128)
            act(v("fp", FW * b + C, FW * b + FW), bank(b, 128, 32), 32.0)
            act(v("hp", FW * b + C, FW * b + FW), bank(b, 128, 32), 64.0 if b < 4 - NG else 0.5)
        sweep(v("s3"), "l3", "x4", 3, PARTS[3], 1.0, 3 * U, "dmax", "s4", A.add, A.max)
        scan(v("e3"), v("de"), v("s3", 2, 3 * C, 3), A.min)
        tt(v("sm", 24, 48), v("m2", 0, 24), lost, A.subtract)
        tt(v("sm", 72, 96), last("e3"), v("sm", 24, 48), A.add)
        tt(v("rp", 1, 48, 2), v("sm", 72, 96), v("sm", 0, 24), A.max)
        for a, b in REPLY:
            i, j = a // 16, b // 16
            scan(v("ti", 2 * i, 2 * j), v("s4", 3 * a + 23, 3 * b, 24), v("rp", 2 * i, 2 * j), A.min)
            ts(v("ti", 48 + i, 48 + j), v("ti", 2 * i + 1, 2 * j, 2), 511, A.bitwise_and)
            cp(v("tl", i, j), v("ti", 48 + i, 48 + j))

        def picked(name, b, lo, hi):
            return [v(name, FW * b, FW * b + FW), v("tl", lo // 16, hi // 16)]

        row[0] = "layer"
        for b in range(4 - NG, 4):
            for lo, hi in (REPLY if b == 4 - NG else ((0, C),)):
                act(v("hp", b * FW + lo, b * FW + hi), picked("fp", b, lo, hi), 1.0 / 64)
        for b in range(SPLIT):
            lo, hi = REPLY[0]
            tt(v("hp", FW * b + lo, FW * b + hi), picked("fp", b, lo, hi), v("fq", C * b + lo, C * b + hi), A.add)
        for b in range(4 - NG):
            for lo, hi in (REPLY[1:] if b < SPLIT else ((0, C),)):
                tt(v("hp", FW * b + lo, FW * b + hi), picked("fp", b, lo, hi), v("fq", C * b + lo, C * b + hi), A.add)
            if b == 1:
                for k in range(4 - NG, 4):
                    for lo, hi in REPLY:
                        o, i = v("fq", k * C + lo, k * C + hi), v("hp", k * FW + lo, k * FW + hi)
                        op("G", lambda o=o, i=i, w=hi - lo: g.affine_select(ap(o), ap(i), [[0, w]], A.is_equal, 0.0, 0, 0), [i], [o])
        for b, lo, hi in ZA:
            act(v("zt", 4 * lo + b, 4 * hi, 4), picked("hp", b, lo, hi), 1.0 / 64)
        for lo, hi in runs:
            for b in range(4 - NG, 4):
                tt(v("zt", 4 * lo + b, 4 * hi, 4), picked("hp", b, lo, hi), v("fq", b * C + lo, b * C + hi), A.add)
        row[0] = None
        if n == ROUNDS - 1:
            act(v("otb"), [v("iw"), v("tl")])
            dma("S", lambda: T.ot[:], lambda: ap(v("otb", 0, C, 1, (0, 128, 16))), [v("otb")], [])

        for i, (lo, hi) in enumerate(runs):
            quant("Z", lo, hi, v("zt", 4 * lo, 4 * hi))
            for b in range(4):
                mm(4 * (i % 2) + b, "W", 128 * b, "Z", lo, hi - lo)
            for b in range(4):
                f, x = v("fp", FW * b + lo, FW * b + hi), v("xt", 4 * lo + b, 4 * hi, 4)
                row[0] = "adds"
                tt(f, bank(4 * (i % 2) + b, hi - lo), f, A.add)
                row[0] = None
                if (i, b) in COPY:
                    ts(x, f, 1.0 / 32, A.mult)
                else:
                    act(x, f, 1.0 / 32)
            quant("X", lo, hi, v("xt", 4 * lo, 4 * hi))
        if n == 0:
            quant("V", 0, 128, v("vt"))
        if n < ROUNDS - 1:
            for b in range(4 - NG):
                twin(b)

    for n in range(ROUNDS):
        a_round(n)

    for i, (lo, hi) in enumerate(runs):
        mm(4 + i, "V", 0, "X", lo, hi - lo)
        (cp if hi == C else act)(v("yb", lo, hi), bank(4 + i, hi - lo))

    def store(q, name, lo, hi):
        if name == "oc":
            dma(q, lambda: T.oc[:, 4 * lo:4 * hi], lambda: codes(v("qX", lo, hi)), [v("qX", lo, hi)], [])
        elif name == "y":
            dma(q, lambda: T.y[:, lo:hi], lambda: ap(v("yb", lo, hi)), [v("yb", lo, hi)], [])
        else:
            dma(q, lambda: T.osc[4 * lo:4 * hi, :], lambda: ap(v("sX", 0, C, 1, (32 * lo, 32 * lo + 4))), [v("sX")], [])
        ops[-1]["far"] = TRIP + 4 * (hi - lo)

    for side in (("S", "oc", 0, CUTS[-2]), ("A", "y", 0, CUTS[-2]), ("S", "oc", CUTS[-2], C), ("S", "osc", 0, 1), ("A", "osc", 1, 2),
                 ("S", "osc", 2, 3), ("A", "osc", 3, 4), ("S", "y", CUTS[-2], C)):
        store(*side)

    names = "VAPGSX"

    def cols(r):
        if r[0] == "ps":
            return slice(r[1] // 512 * 512, r[1] // 512 * 512 + 512)
        return slice(r[1], r[2], r[3])

    def needs():
        wrote = {b: np.full(s[1][1], -1) for b, s in SCRATCH.items()}
        read = {b: [] for b in SCRATCH}
        out = []
        for i, o in enumerate(ops):
            deps = set()
            for r in o["r"] + o["w"]:
                deps.update(int(d) for d in np.unique(wrote[r[0]][cols(r)]))
            for r in o["w"] + [r for r in o["r"] if r[0] == "ps"]:
                mark = np.zeros(SCRATCH[r[0]][1][1], bool)
                mark[cols(r)] = True
                deps.update(d for d, c in read[r[0]] if mark[c].any() and (r in o["w"] or ops[d]["q"] != o["q"]))
            for r in o["w"]:
                wrote[r[0]][cols(r)] = i
                read[r[0]] = [(d, c) for d, c in read[r[0]] if (wrote[r[0]][c] < d).any()]
            if o["k"] != "remote":
                for r in o["r"]:
                    read[r[0]].append((i, cols(r)))
            out.append(deps - {-1, i})
        return out

    def length(o):
        if o["k"] != "c":
            wide = sum(len(range(*r[1:4])) for r in o["w"])
            return (300, 0) if o["k"] == "remote" else (50, o.get("far", TRIP + wide))
        n = max(len(range(*r[1:4])) for r in o["w"] + o["r"][-1:] * o["s"])
        sides = [SCRATCH[r[0]] for r in o["w"] + o["r"] if len(range(*r[1:4])) > 1]
        if any(SCRATCH[r[0]][2] == U16 for r in o["r"]) and sides[0][2] != U16:
            return 60 + n * (2.8 if o["s"] else 1.25), 0
        if o["q"] == "V" and sides and all(s[2] == BF for s in sides):
            n = n / 2
        return {"V": max(64, n) * 0.83, "A": 50 + max(64, n) * 0.83, "P": 0.6 * n + 10, "G": 150 + 1.66 * n}[o["q"]], 150 * (o["q"] == "P")

    deps, true = needs(), needs()
    for i, o in enumerate(ops):
        if o["q"] in "GSX" or o["k"] == "dma":
            deps[i].update([j for j in range(i) if ops[j]["q"] == o["q"] or ops[j]["k"] == "remote"][-1:])
        if o["row"]:
            deps[i].update([j for j in range(i) if ops[j]["q"] == o["q"] and ops[j]["row"] == o["row"]][-1:])
    size = [length(o) for o in ops]
    after = [set() for o in ops]
    for i in range(len(ops)):
        for d in deps[i]:
            after[d].add(i)

    def lag(d, i):
        return size[d][1] + WAKE if ops[d]["k"] != "remote" and ops[i]["q"] != ops[d]["q"] or (d in true[i] and ops[i]["q"] != "P") else 0

    def place(order, before, gap):
        busy, end = {q: [] for q in names}, {}
        for i in order:
            t = max([size[i][1] if before is after else 0.0] + [end[d] + gap(d, i) for d in before[i]])
            line, k = busy[ops[i]["q"]], 0
            while k < len(line) and line[k][0] < t + size[i][0]:
                t = max(t, line[k][1])
                k += 1
            line.insert(k, (t, t + size[i][0]))
            end[i] = t + size[i][0]
        return end

    ahead = [0.0] * len(ops)
    for i in range(len(ops) - 1, -1, -1):
        ahead[i] = sum(size[i]) + max([0.0] + [ahead[j] + lag(i, j) - size[i][1] for j in after[i]])
    end = place(sorted(range(len(ops)), key=lambda i: (-ahead[i], i)), deps, lag)
    for _ in range(TURNS):
        back = place(sorted(range(len(ops)), key=lambda i: (-end[i], -i)), after, lambda d, i: lag(i, d))
        end = place(sorted(range(len(ops)), key=lambda i: (-back[i], i)), deps, lag)
    ops[:] = [ops[i] for i in sorted(range(len(ops)), key=lambda i: (end[i] - size[i][0], i))]

    deps = needs()
    known = {q: {} for q in names}
    done, waits, waited = [], [], set()

    def source(d):
        return ops[d]["q"] if ops[d]["k"] == "c" else ops[d]["sem"]

    for i, o in enumerate(ops):
        q, mine = o["q"], []
        for d in sorted(deps[i], reverse=True):
            if q != "X" and not ops[d]["q"] == q == "P" and known[q].get(source(d), -1) < d:
                mine.append(d)
                waited.add(d)
                for s, w in done[d].items():
                    known[q][s] = max(known[q].get(s, -1), w)
        waits.append(mine)
        done.append(dict(known[q]))
        if o["k"] != "remote":
            done[i][source(i)] = i

    count, total = {}, {q: 0 for q in names}
    for i, o in enumerate(ops):
        if o["k"] == "c" and i in waited:
            total[o["q"]] += 1
            count[i] = total[o["q"]]
    for i, o in enumerate(ops):
        for d in waits[i]:
            if ops[d]["k"] == "c":
                queue[o["q"]].wait_ge(T.sem["c" + ops[d]["q"]], count[d])
            else:
                queue[o["q"]].wait_ge(T.sem[ops[d]["sem"]], ops[d]["n"])
        if o["q"] == "X":
            continue
        ins = o["f"]()
        if o["k"] == "dma":
            ins.then_inc(T.sem[o["sem"]], 16)
        elif i in waited:
            ins.then_inc(T.sem["c" + o["q"]], 1)
    g.wait_ge(T.sem.sent, 2 * len(lanes(core, dest)) * ROUNDS)
    for i, o in enumerate(ops):
        if o["k"] == "dma" and i not in waited:
            queue[o["q"]].wait_ge(T.sem[o["sem"]], o["n"])
